import numpy as np
import ml_dtypes


def mxq(x, axis, fmt="e4m3"):
    dtype, down = {"e4m3": (ml_dtypes.float8_e4m3fn, 7), "e5m2": (ml_dtypes.float8_e5m2, 14)}[fmt]
    v = np.moveaxis(np.asarray(x, np.float32).astype(ml_dtypes.bfloat16).astype(np.float64), axis, -1)
    blocks = v.reshape(v.shape[:-1] + (-1, 32))
    amax = np.abs(blocks).max(-1, keepdims=True)
    byte = np.maximum(np.where(amax > 0, np.frexp(amax)[1] - 1 + 127, 0) - down, 1)
    scale = np.exp2(byte - 127.0)
    codes = (blocks / scale).astype(np.float32).astype(dtype).astype(np.float64)
    return np.moveaxis((codes * scale).reshape(v.shape), -1, axis)


WIDE = False


def mx_kscale(k):
    if not WIDE:
        return np.ones(k)
    levels = np.array([10, -10, 5, -5, 0])
    if k % 512:
        return np.exp2(np.random.permutation(np.resize(levels, k // 32))).repeat(32)
    a = np.empty((k // 512, 16))
    for p in range(k // 512):
        a[p, :8] = np.random.permutation(np.resize(levels, 8))
        for g in range(8):
            far = levels[np.abs(levels - a[p, g]) >= 10]
            a[p, g + 8] = far[np.random.randint(len(far))]
    return np.exp2(a.ravel()).repeat(32)


def f64(x):
    return np.asarray(x).astype(np.float64)


def striped(idx):
    return np.tile(idx.reshape(-1, 16).T, (8, 1)).astype(np.uint16)


def unstriped(offs):
    return offs[:16].T.reshape(-1).astype(np.int64)


def pack_weight(w):
    k, n = w.shape
    w = f64(np.asarray(w, np.float32).astype(ml_dtypes.bfloat16)).reshape(k // 32, 32, n)
    amax = np.abs(w).max(1)
    byte = np.clip(np.where(amax > 0, np.frexp(amax)[1] - 1 + 127 - 7, 1), 1, 254)
    scaled = (w * np.exp2(127.0 - byte)[:, None, :]).reshape(k, n).astype(np.float32)
    words = np.ascontiguousarray(scaled.reshape(k // 512, 128, 4, n).transpose(0, 1, 3, 2)).astype(ml_dtypes.float8_e4m3fn).view(np.uint8)
    return words, np.ascontiguousarray(byte.astype(np.uint8).reshape(k // 512, 16, n))


def unpack_weight(words, scales):
    g, p, n, _ = words.shape
    vals = np.ascontiguousarray(words).view(ml_dtypes.float8_e4m3fn).astype(np.float64) * np.repeat(np.exp2(scales.astype(np.float64) - 127.0), 8, axis=1)[..., None]
    return vals.transpose(0, 1, 3, 2).reshape(g * 512, n)


def sigmoid(v):
    return 1.0 / (1.0 + np.exp(-np.maximum(v, -700.0)))


K, T, S, H, D, V, W, U = 512, 2048, 512, 512, 4, 128, 1024, 512


def setup_inputs():
    n = np.random.standard_normal
    s = mx_kscale(K)[:, None]
    u = mx_kscale(H)
    packed_xT = pack_weight(n((K, T)) * s)
    packed_eT = pack_weight(n((H, W)) / np.sqrt(H) / u[:, None])
    return {
        "x_words": packed_xT[0],
        "x_scales": packed_xT[1],
        "w1": (n((K, H)) / np.sqrt(K) / s * u).astype(np.float32),
        "e_words": packed_eT[0],
        "e_scales": packed_eT[1],
        "pos": (n((S, V))).astype(np.float32),
        "offs": striped(np.random.permutation(T)[:S]),
        "neg": striped(np.random.permutation(W)[:U]),
    }


def reference(x_words, x_scales, w1, e_words, e_scales, pos, offs, neg):
    xq = unpack_weight(x_words, x_scales)[:, unstriped(offs)]
    h = mxq(f64(w1), 0, "e4m3").T @ xq
    e_neg = unpack_weight(e_words, e_scales)[:, unstriped(neg)]
    y = mxq(h, 0, "e4m3").T @ e_neg
    top = y.reshape(len(y), -1, D).max(axis=2)
    ex = np.exp(y - np.repeat(top, D, axis=1))
    total = ex.reshape(len(ex), -1, D).sum(axis=2)
    wgt = ex / np.repeat(total, D, axis=1)
    sp = np.repeat(f64(pos), D, axis=1)
    z = wgt * sigmoid(sp - y)
    return -1.0 * (np.log(z.reshape(len(z), -1, D).sum(axis=2) + 1e-3))

@@ -1,0 +1,190 @@
+import math
+from contextlib import ExitStack
+
+import concourse.mybir as mybir
+from concourse.masks import make_identity
+
+K, T, S, H, D, V, W, U = 512, 2048, 512, 512, 4, 128, 1024, 512
+FLOPS = 2 * K * H * S + 2 * H * S * U
+
+F32 = mybir.dt.float32
+BF16 = mybir.dt.bfloat16
+I32 = mybir.dt.int32
+U32 = mybir.dt.uint32
+U16 = mybir.dt.uint16
+U8 = mybir.dt.uint8
+FP8X4 = mybir.dt.float8_e4m3fn_x4
+ALU = mybir.AluOpType
+ACT = mybir.ActivationFunctionType
+
+P = 128
+PACK = 4
+BLOCKS = S // P
+REACH = 32.0
+EPS = 1e-3
+M_SCALAR = 80
+
+
+def load_scale_rows(engines, plane, scales):
+    rows = scales[0].rearrange("(q r) c -> r q c", r=4)
+    for r, engine in enumerate(engines):
+        engine.dma_start(out=plane[r:P:32, :].bitcast(I32), in_=rows[r].bitcast(I32))
+
+
+def tile_picked_ytop1_bpr_p_kernel(
+    tc, x_words, x_scales, w1, e_words, e_scales, pos, offs, neg, out
+):
+    nc = tc.nc
+    with ExitStack() as ctx:
+        keep = ctx.enter_context(tc.tile_pool(name="keep", bufs=1))
+        psum = ctx.enter_context(tc.psum_pool(name="psum", bufs=1))
+
+        offs_t = keep.tile([P, S // 16], U16, name="offs_t")
+        neg_t = keep.tile([P, U // 16], U16, name="neg_t")
+        w_raw = keep.tile([P, PACK, H], F32, name="w_raw")
+        x_tab = keep.tile([P, T], U32, name="x_tab", align_bytes=64)
+        xs_tab = keep.tile([P, T], U8, name="xs_tab", tag="xs", align_bytes=64)
+        e_tab = keep.tile([P, W], U32, name="e_tab", align_bytes=64)
+        es_tab = keep.tile([P, W], U8, name="es_tab", tag="es", align_bytes=64)
+        ident = keep.tile([P, P], F32, name="ident")
+
+        nc.vector.memset(xs_tab[:].bitcast(I32), 0)
+        nc.vector.memset(es_tab[:].bitcast(I32), 0)
+        nc.sync.dma_start(offs_t[:], offs)
+        nc.sync.dma_start(neg_t[:], neg)
+        load_scale_rows([nc.scalar, nc.scalar, nc.scalar, nc.gpsimd], xs_tab, x_scales)
+        nc.sync.dma_start(out=w_raw[:], in_=w1.rearrange("(p j) c -> p j c", j=PACK))
+        load_scale_rows([nc.gpsimd] * 4, es_tab, e_scales)
+        nc.sync.dma_start(out=x_tab[:].bitcast(I32), in_=x_words[0].rearrange("p n t -> p (n t)").bitcast(I32))
+        nc.sync.dma_start(out=e_tab[:].bitcast(I32), in_=e_words[0].rearrange("p n t -> p (n t)").bitcast(I32))
+        make_identity(nc, ident[:])
+
+        x_sc = keep.tile([P, S], U8, name="x_sc", align_bytes=64)
+        nc.vector.tensor_copy(x_sc[:], xs_tab[:].indirect(offs_t[:]))
+        pos_sb = keep.tile([P, BLOCKS, V], F32, name="pos_sb", tag="xs", align_bytes=64)
+        nc.sync.dma_start(out=pos_sb[:], in_=pos.rearrange("(b p) v -> p b v", p=P))
+
+        w_bf = keep.tile([P, PACK * H], BF16, name="w_bf", align_bytes=64)
+        w_dst = w_bf[:].rearrange("p (t m j) -> p m t j", t=PACK, j=PACK)
+        w_src = w_raw[:].rearrange("p j (m t) -> p m t j", t=PACK)
+        nc.scalar.activation(out=w_dst[:, :M_SCALAR], in_=w_src[:, :M_SCALAR], func=ACT.Copy)
+        nc.vector.tensor_copy(out=w_dst[:, M_SCALAR:], in_=w_src[:, M_SCALAR:])
+
+        e_sc_list = keep.tile([P, U], U8, name="e_sc_list", align_bytes=64)
+        nc.vector.tensor_copy(e_sc_list[:], es_tab[:].indirect(neg_t[:]))
+        e_sc = keep.tile([P, U], U8, name="e_sc", align_bytes=64)
+        nc.vector.tensor_copy(
+            out=e_sc[:].rearrange("p (d v) -> p d v", d=D),
+            in_=e_sc_list[:].rearrange("p (v d) -> p d v", d=D),
+        )
+
+        w_q = keep.tile([P, H], U32, name="w_q", align_bytes=64)
+        w_sc = keep.tile([P, H], U8, name="w_sc", align_bytes=64)
+        nc.vector.quantize_mx(out=w_q[:].bitcast(FP8X4), scales=w_sc[:], in_=w_bf[:])
+
+        half = S // 2
+        x_q = [keep.tile([P, half], U32, name="x_q%d" % a, tag=["es", "x_q1"][a], align_bytes=64) for a in range(2)]
+        for a in range(2):
+            nc.vector.tensor_copy(x_q[a][:], x_tab[:].indirect(offs_t[:, a * half // 16 : (a + 1) * half // 16]))
+        e_q = keep.tile([P, U], U32, name="e_q", align_bytes=64)
+        nc.vector.tensor_copy(e_q[:].rearrange("p (d v) -> p v d", d=D), e_tab[:].indirect(neg_t[:]))
+
+        h_q = [keep.tile([P, P], U32, name="h_q%d" % b, align_bytes=64) for b in range(BLOCKS)]
+        h_sc = [keep.tile([P, P], U8, name="h_sc%d" % b, align_bytes=64) for b in range(BLOCKS)]
+
+        def hidden(b):
+            h_ps = psum.tile([P, PACK, P], F32, name="h_ps%d" % b, tag=["ha", "hb", "hc", "hb"][b])
+            cols = slice((b % 2) * P, (b % 2 + 1) * P)
+            for t in range(PACK):
+                wc = slice(t * P, (t + 1) * P)
+                nc.tensor.matmul_mx(
+                    out=h_ps[:, t, :],
+                    lhsT=w_q[:, wc].bitcast(FP8X4),
+                    lhsT_scale=w_sc[:, wc],
+                    rhs=x_q[b // 2][:, cols].bitcast(FP8X4),
+                    rhs_scale=x_sc[:, b * P : (b + 1) * P],
+                    start=True,
+                    stop=True,
+                )
+            h_bf = keep.tile([P, P, PACK], BF16, name="h_bf%d" % b, align_bytes=64)
+            nc.scalar.copy(out=h_bf[:], in_=h_ps[:].rearrange("p t n -> p n t"))
+            nc.vector.quantize_mx(
+                out=h_q[b][:].bitcast(FP8X4), scales=h_sc[b][:], in_=h_bf[:].rearrange("p n t -> p (n t)")
+            )
+
+        u = [keep.tile([P, D, P], F32, name="u%d" % b) for b in range(BLOCKS)]
+        ex = [keep.tile([P, D, P], F32, name="ex%d" % b) for b in range(BLOCKS)]
+        th = [keep.tile([P, D, P], F32, name="th%d" % b) for b in range(BLOCKS)]
+        sums = [psum.tile([P, 2, 2, V], F32, name="sums%d" % a) for a in range(2)]
+
+        def scores(b):
+            y_ps = psum.tile([P, D, P], F32, name="y_ps", bufs=3)
+            for d in range(D):
+                ec = slice(d * P, (d + 1) * P)
+                nc.tensor.matmul_mx(
+                    out=y_ps[:, d, :],
+                    lhsT=e_q[:, ec].bitcast(FP8X4),
+                    lhsT_scale=e_sc[:, ec],
+                    rhs=h_q[b][:].bitcast(FP8X4),
+                    rhs_scale=h_sc[b][:],
+                    start=True,
+                    stop=True,
+                )
+            top = keep.tile([P, P], F32, name="top%d" % b)
+            nc.vector.tensor_reduce(
+                out=top[:], in_=y_ps[:].rearrange("p d t -> p t d"), axis=mybir.AxisListType.X, op=ALU.max
+            )
+            capped = keep.tile([P, P], F32, name="capped%d" % b)
+            nc.vector.scalar_tensor_tensor(capped[:], top[:], REACH, pos_t[:, b, :], ALU.add, ALU.min)
+            shift = keep.tile([P, P], F32, name="shift%d" % b)
+            nc.vector.scalar_tensor_tensor(shift[:], top[:], -REACH, capped[:], ALU.add, ALU.max)
+            nc.vector.tensor_tensor(
+                u[b][:], y_ps[:], shift[:].unsqueeze(1).to_broadcast([P, D, P]), ALU.subtract
+            )
+            nc.scalar.activation(out=ex[b][:], in_=u[b][:], func=ACT.Exp)
+            nc.scalar.activation(out=th[b][:], in_=u[b][:], func=ACT.Tanh, scale=-0.5)
+
+        def add_turned(dst, src):
+            for d in range(D):
+                nc.tensor.matmul(dst, src[:, d, :], ident[:], start=(d == 0), stop=(d == D - 1), is_transpose=True)
+
+        def weigh(b):
+            wt = keep.tile([P, D, P], F32, name="wt%d" % b)
+            nc.vector.scalar_tensor_tensor(
+                wt[:].rearrange("p d t -> p (d t)"),
+                th[b][:].rearrange("p d t -> p (d t)"),
+                1.0 + 2.0 * EPS,
+                ex[b][:].rearrange("p d t -> p (d t)"),
+                ALU.add,
+                ALU.mult,
+            )
+            add_turned(sums[b // 2][:, b % 2, 1, :], wt)
+
+        hidden(0)
+        hidden(1)
+        pos_t = psum.tile([P, BLOCKS, P], F32, name="pos_t", tag="ha")
+        for b in range(BLOCKS):
+            nc.tensor.transpose(pos_t[:, b, :], pos_sb[:, b, :], ident[:])
+        for b in range(BLOCKS):
+            scores(b)
+            if b + 2 < BLOCKS:
+                hidden(b + 2)
+            if b >= 1:
+                add_turned(sums[(b - 1) // 2][:, (b - 1) % 2, 0, :], ex[b - 1])
+        add_turned(sums[1][:, 1, 0, :], ex[BLOCKS - 1])
+        for b in range(BLOCKS):
+            weigh(b)
+
+        out_rows = out.rearrange("(b p) v -> p b v", p=P)
+        for a in range(2):
+            logs = u[BLOCKS - 1 - a][:].rearrange("p (i k) v -> p i k v", k=2)
+            nc.scalar.activation(
+                out=logs.rearrange("p i k v -> p (i k v)"),
+                in_=sums[a][:].rearrange("p i k v -> p (i k v)"),
+                func=ACT.Ln,
+            )
+            res = keep.tile([P, 2, V], F32, name="res%d" % a)
+            nc.vector.scalar_tensor_tensor(
+                res[:], logs[:, :, 0, :], math.log(2.0), logs[:, :, 1, :], ALU.add, ALU.subtract
+            )
+            nc.sync.dma_start(out=out_rows[:, 2 * a : 2 * a + 2, :], in_=res[:])

@@ -22,7 +22,8 @@ PACK = 4
 BLOCKS = S // P
 REACH = 32.0
 EPS = 1e-3
-M_SCALAR = 80
+FLOOR = 2.0**-50
+M_SCALAR = 96
 
 
 def load_scale_rows(engines, plane, scales):
@@ -48,27 +49,21 @@ def tile_picked_ytop1_bpr_p_kernel(
         es_tab = keep.tile([P, W], U8, name="es_tab", tag="es", align_bytes=64)
         ident = keep.tile([P, P], F32, name="ident")
 
-        nc.vector.memset(xs_tab[:].bitcast(I32), 0)
-        nc.vector.memset(es_tab[:].bitcast(I32), 0)
-        nc.sync.dma_start(offs_t[:], offs)
+        pos_sb = keep.tile([P, BLOCKS, V], F32, name="pos_sb")
+        for plane in (es_tab, xs_tab):
+            words = plane[:].bitcast(I32)
+            mid = words.shape[1] // 2
+            nc.gpsimd.memset(words[:, :mid], 0)
+            nc.vector.memset(words[:, mid:], 0)
         nc.sync.dma_start(neg_t[:], neg)
-        load_scale_rows([nc.scalar, nc.scalar, nc.scalar, nc.gpsimd], xs_tab, x_scales)
+        nc.sync.dma_start(offs_t[:], offs)
+        load_scale_rows([nc.sync] * 4, es_tab, e_scales)
         nc.sync.dma_start(out=w_raw[:], in_=w1.rearrange("(p j) c -> p j c", j=PACK))
-        load_scale_rows([nc.gpsimd] * 4, es_tab, e_scales)
+        load_scale_rows([nc.sync] * 4, xs_tab, x_scales)
         nc.sync.dma_start(out=x_tab[:].bitcast(I32), in_=x_words[0].rearrange("p n t -> p (n t)").bitcast(I32))
         nc.sync.dma_start(out=e_tab[:].bitcast(I32), in_=e_words[0].rearrange("p n t -> p (n t)").bitcast(I32))
-        make_identity(nc, ident[:])
-
-        x_sc = keep.tile([P, S], U8, name="x_sc", align_bytes=64)
-        nc.vector.tensor_copy(x_sc[:], xs_tab[:].indirect(offs_t[:]))
-        pos_sb = keep.tile([P, BLOCKS, V], F32, name="pos_sb", tag="xs", align_bytes=64)
         nc.sync.dma_start(out=pos_sb[:], in_=pos.rearrange("(b p) v -> p b v", p=P))
-
-        w_bf = keep.tile([P, PACK * H], BF16, name="w_bf", align_bytes=64)
-        w_dst = w_bf[:].rearrange("p (t m j) -> p m t j", t=PACK, j=PACK)
-        w_src = w_raw[:].rearrange("p j (m t) -> p m t j", t=PACK)
-        nc.scalar.activation(out=w_dst[:, :M_SCALAR], in_=w_src[:, :M_SCALAR], func=ACT.Copy)
-        nc.vector.tensor_copy(out=w_dst[:, M_SCALAR:], in_=w_src[:, M_SCALAR:])
+        make_identity(nc, ident[:])
 
         e_sc_list = keep.tile([P, U], U8, name="e_sc_list", align_bytes=64)
         nc.vector.tensor_copy(e_sc_list[:], es_tab[:].indirect(neg_t[:]))
@@ -77,13 +72,21 @@ def tile_picked_ytop1_bpr_p_kernel(
             out=e_sc[:].rearrange("p (d v) -> p d v", d=D),
             in_=e_sc_list[:].rearrange("p (v d) -> p d v", d=D),
         )
+        x_sc = keep.tile([P, S], U8, name="x_sc", align_bytes=64)
+        nc.vector.tensor_copy(x_sc[:], xs_tab[:].indirect(offs_t[:]))
+
+        w_bf = keep.tile([P, PACK * H], BF16, name="w_bf", align_bytes=64)
+        w_dst = w_bf[:].rearrange("p (t m j) -> p m t j", t=PACK, j=PACK)
+        w_src = w_raw[:].rearrange("p j (m t) -> p m t j", t=PACK)
+        nc.scalar.activation(out=w_dst[:, :M_SCALAR], in_=w_src[:, :M_SCALAR], func=ACT.Copy)
+        nc.vector.tensor_copy(out=w_dst[:, M_SCALAR:], in_=w_src[:, M_SCALAR:])
 
         w_q = keep.tile([P, H], U32, name="w_q", align_bytes=64)
         w_sc = keep.tile([P, H], U8, name="w_sc", align_bytes=64)
         nc.vector.quantize_mx(out=w_q[:].bitcast(FP8X4), scales=w_sc[:], in_=w_bf[:])
 
         half = S // 2
-        x_q = [keep.tile([P, half], U32, name="x_q%d" % a, tag=["es", "x_q1"][a], align_bytes=64) for a in range(2)]
+        x_q = [keep.tile([P, half], U32, name="x_q%d" % a, align_bytes=64) for a in range(2)]
         for a in range(2):
             nc.vector.tensor_copy(x_q[a][:], x_tab[:].indirect(offs_t[:, a * half // 16 : (a + 1) * half // 16]))
         e_q = keep.tile([P, U], U32, name="e_q", align_bytes=64)
@@ -115,7 +118,8 @@ def tile_picked_ytop1_bpr_p_kernel(
         u = [keep.tile([P, D, P], F32, name="u%d" % b) for b in range(BLOCKS)]
         ex = [keep.tile([P, D, P], F32, name="ex%d" % b) for b in range(BLOCKS)]
         th = [keep.tile([P, D, P], F32, name="th%d" % b) for b in range(BLOCKS)]
-        sums = [psum.tile([P, 2, 2, V], F32, name="sums%d" % a) for a in range(2)]
+        sum_ex = psum.tile([P, BLOCKS, V], F32, name="sum_ex")
+        sum_wt = psum.tile([P, BLOCKS, V], F32, name="sum_wt")
 
         def scores(b):
             y_ps = psum.tile([P, D, P], F32, name="y_ps", bufs=3)
@@ -134,10 +138,8 @@ def tile_picked_ytop1_bpr_p_kernel(
             nc.vector.tensor_reduce(
                 out=top[:], in_=y_ps[:].rearrange("p d t -> p t d"), axis=mybir.AxisListType.X, op=ALU.max
             )
-            capped = keep.tile([P, P], F32, name="capped%d" % b)
-            nc.vector.scalar_tensor_tensor(capped[:], top[:], REACH, pos_t[:, b, :], ALU.add, ALU.min)
-            shift = keep.tile([P, P], F32, name="shift%d" % b)
-            nc.vector.scalar_tensor_tensor(shift[:], top[:], -REACH, capped[:], ALU.add, ALU.max)
+            shift = keep.tile([P, P], F32, name="shift%d" % b, tag="shift%d" % b)
+            nc.vector.scalar_tensor_tensor(shift[:], top[:], -REACH, pos_t[:, b, :], ALU.add, ALU.max)
             nc.vector.tensor_tensor(
                 u[b][:], y_ps[:], shift[:].unsqueeze(1).to_broadcast([P, D, P]), ALU.subtract
             )
@@ -149,16 +151,16 @@ def tile_picked_ytop1_bpr_p_kernel(
                 nc.tensor.matmul(dst, src[:, d, :], ident[:], start=(d == 0), stop=(d == D - 1), is_transpose=True)
 
         def weigh(b):
-            wt = keep.tile([P, D, P], F32, name="wt%d" % b)
+            wt = wt_all[:, b]
             nc.vector.scalar_tensor_tensor(
-                wt[:].rearrange("p d t -> p (d t)"),
+                wt.rearrange("p d t -> p (d t)"),
                 th[b][:].rearrange("p d t -> p (d t)"),
                 1.0 + 2.0 * EPS,
                 ex[b][:].rearrange("p d t -> p (d t)"),
                 ALU.add,
                 ALU.mult,
             )
-            add_turned(sums[b // 2][:, b % 2, 1, :], wt)
+            add_turned(sum_wt[:, b, :], wt)
 
         hidden(0)
         hidden(1)
@@ -170,21 +172,23 @@ def tile_picked_ytop1_bpr_p_kernel(
             if b + 2 < BLOCKS:
                 hidden(b + 2)
             if b >= 1:
-                add_turned(sums[(b - 1) // 2][:, (b - 1) % 2, 0, :], ex[b - 1])
-        add_turned(sums[1][:, 1, 0, :], ex[BLOCKS - 1])
+                add_turned(sum_ex[:, b - 1, :], ex[b - 1])
+        add_turned(sum_ex[:, BLOCKS - 1, :], ex[BLOCKS - 1])
+        wt_all = keep.tile([P, BLOCKS, D, P], F32, name="wt_all", tag="shift%d" % (BLOCKS - 1))
         for b in range(BLOCKS):
             weigh(b)
 
         out_rows = out.rearrange("(b p) v -> p b v", p=P)
+        log_ex = u[BLOCKS - 1]
+        nc.scalar.activation(out=log_ex[:], in_=sum_ex[:], func=ACT.Ln, bias=FLOOR)
+        log_wt = u[BLOCKS - 2]
         for a in range(2):
-            logs = u[BLOCKS - 1 - a][:].rearrange("p (i k) v -> p i k v", k=2)
+            pair = slice(2 * a, 2 * a + 2)
             nc.scalar.activation(
-                out=logs.rearrange("p i k v -> p (i k v)"),
-                in_=sums[a][:].rearrange("p i k v -> p (i k v)"),
-                func=ACT.Ln,
+                out=log_wt[:, pair, :], in_=sum_wt[:, pair, :], func=ACT.Ln, scale=0.5 / (1.0 + EPS), bias=FLOOR
             )
             res = keep.tile([P, 2, V], F32, name="res%d" % a)
             nc.vector.scalar_tensor_tensor(
-                res[:], logs[:, :, 0, :], math.log(2.0), logs[:, :, 1, :], ALU.add, ALU.subtract
+                res[:], log_ex[:, pair, :], -math.log(1.0 + EPS), log_wt[:, pair, :], ALU.add, ALU.subtract
             )
-            nc.sync.dma_start(out=out_rows[:, 2 * a : 2 * a + 2, :], in_=res[:])
+            nc.sync.dma_start(out=out_rows[:, pair, :], in_=res[:])

@@ -23,7 +23,7 @@ BLOCKS = S // P
 REACH = 32.0
 EPS = 1e-3
 FLOOR = 2.0**-50
-M_SCALAR = 96
+M_SCALAR = 64
 
 
 def load_scale_rows(engines, plane, scales):
@@ -45,7 +45,7 @@ def tile_picked_ytop1_bpr_p_kernel(
         w_raw = keep.tile([P, PACK, H], F32, name="w_raw")
         x_tab = keep.tile([P, T], U32, name="x_tab", align_bytes=64)
         xs_tab = keep.tile([P, T], U8, name="xs_tab", tag="xs", align_bytes=64)
-        e_tab = keep.tile([P, W], U32, name="e_tab", align_bytes=64)
+        e_tab = keep.tile([P, W], U32, name="e_tab", tag="h_q0", align_bytes=64)
         es_tab = keep.tile([P, W], U8, name="es_tab", tag="es", align_bytes=64)
         ident = keep.tile([P, P], F32, name="ident")
 
@@ -72,28 +72,39 @@ def tile_picked_ytop1_bpr_p_kernel(
             out=e_sc[:].rearrange("p (d v) -> p d v", d=D),
             in_=e_sc_list[:].rearrange("p (v d) -> p d v", d=D),
         )
-        x_sc = keep.tile([P, S], U8, name="x_sc", align_bytes=64)
-        nc.vector.tensor_copy(x_sc[:], xs_tab[:].indirect(offs_t[:]))
-
         w_bf = keep.tile([P, PACK * H], BF16, name="w_bf", align_bytes=64)
         w_dst = w_bf[:].rearrange("p (t m j) -> p m t j", t=PACK, j=PACK)
         w_src = w_raw[:].rearrange("p j (m t) -> p m t j", t=PACK)
         nc.scalar.activation(out=w_dst[:, :M_SCALAR], in_=w_src[:, :M_SCALAR], func=ACT.Copy)
         nc.vector.tensor_copy(out=w_dst[:, M_SCALAR:], in_=w_src[:, M_SCALAR:])
 
+        half = S // 2
+        offs_half = [offs_t[:, a * half // 16 : (a + 1) * half // 16] for a in range(2)]
+        x_sc = [keep.tile([P, half], U8, name="x_sc%d" % a, align_bytes=64) for a in range(2)]
+        nc.vector.tensor_copy(x_sc[0][:], xs_tab[:].indirect(offs_half[0]))
+
         w_q = keep.tile([P, H], U32, name="w_q", align_bytes=64)
         w_sc = keep.tile([P, H], U8, name="w_sc", align_bytes=64)
         nc.vector.quantize_mx(out=w_q[:].bitcast(FP8X4), scales=w_sc[:], in_=w_bf[:])
 
-        half = S // 2
-        x_q = [keep.tile([P, half], U32, name="x_q%d" % a, align_bytes=64) for a in range(2)]
-        for a in range(2):
-            nc.vector.tensor_copy(x_q[a][:], x_tab[:].indirect(offs_t[:, a * half // 16 : (a + 1) * half // 16]))
+        x_q = []
+
+        def gather_x(a, tag):
+            words = keep.tile([P, half], U32, name="x_q%d" % a, tag=tag, align_bytes=64)
+            nc.vector.tensor_copy(words[:], x_tab[:].indirect(offs_half[a]))
+            x_q.append(words)
+
+        nc.vector.tensor_copy(x_sc[1][:], xs_tab[:].indirect(offs_half[1]))
+        gather_x(0, "x_q0")
+        gather_x(1, "x_q1")
         e_q = keep.tile([P, U], U32, name="e_q", align_bytes=64)
         nc.vector.tensor_copy(e_q[:].rearrange("p (d v) -> p v d", d=D), e_tab[:].indirect(neg_t[:]))
 
-        h_q = [keep.tile([P, P], U32, name="h_q%d" % b, align_bytes=64) for b in range(BLOCKS)]
+        h_q = [keep.tile([P, P], U32, name="h_q%d" % b, tag="h_q%d" % b, align_bytes=64) for b in range(BLOCKS)]
         h_sc = [keep.tile([P, P], U8, name="h_sc%d" % b, align_bytes=64) for b in range(BLOCKS)]
+
+        h_bf = {}
+        y_ps = {}
 
         def hidden(b):
             h_ps = psum.tile([P, PACK, P], F32, name="h_ps%d" % b, tag=["ha", "hb", "hc", "hb"][b])
@@ -105,28 +116,22 @@ def tile_picked_ytop1_bpr_p_kernel(
                     lhsT=w_q[:, wc].bitcast(FP8X4),
                     lhsT_scale=w_sc[:, wc],
                     rhs=x_q[b // 2][:, cols].bitcast(FP8X4),
-                    rhs_scale=x_sc[:, b * P : (b + 1) * P],
+                    rhs_scale=x_sc[b // 2][:, cols],
                     start=True,
                     stop=True,
                 )
-            h_bf = keep.tile([P, P, PACK], BF16, name="h_bf%d" % b, align_bytes=64)
-            nc.scalar.copy(out=h_bf[:], in_=h_ps[:].rearrange("p t n -> p n t"))
-            nc.vector.quantize_mx(
-                out=h_q[b][:].bitcast(FP8X4), scales=h_sc[b][:], in_=h_bf[:].rearrange("p n t -> p (n t)")
-            )
-
-        u = [keep.tile([P, D, P], F32, name="u%d" % b) for b in range(BLOCKS)]
-        ex = [keep.tile([P, D, P], F32, name="ex%d" % b) for b in range(BLOCKS)]
-        th = [keep.tile([P, D, P], F32, name="th%d" % b) for b in range(BLOCKS)]
-        sum_ex = psum.tile([P, BLOCKS, V], F32, name="sum_ex")
-        sum_wt = psum.tile([P, BLOCKS, V], F32, name="sum_wt")
+            h_bf[b] = keep.tile([P, P, PACK], BF16, name="h_bf%d" % b, tag="h_bf%d" % b, align_bytes=64)
+            nc.scalar.copy(out=h_bf[b][:], in_=h_ps[:].rearrange("p t n -> p n t"))
 
         def scores(b):
-            y_ps = psum.tile([P, D, P], F32, name="y_ps", bufs=3)
+            nc.vector.quantize_mx(
+                out=h_q[b][:].bitcast(FP8X4), scales=h_sc[b][:], in_=h_bf[b][:].rearrange("p n t -> p (n t)")
+            )
+            y_ps[b] = psum.tile([P, D, P], F32, name="y_ps%d" % b, tag=["ya", "yb", "yc", "hc"][b])
             for d in range(D):
                 ec = slice(d * P, (d + 1) * P)
                 nc.tensor.matmul_mx(
-                    out=y_ps[:, d, :],
+                    out=y_ps[b][:, d, :],
                     lhsT=e_q[:, ec].bitcast(FP8X4),
                     lhsT_scale=e_sc[:, ec],
                     rhs=h_q[b][:].bitcast(FP8X4),
@@ -134,14 +139,24 @@ def tile_picked_ytop1_bpr_p_kernel(
                     start=True,
                     stop=True,
                 )
-            top = keep.tile([P, P], F32, name="top%d" % b)
+
+        u = [keep.tile([P, D, P], F32, name="u%d" % b) for b in range(BLOCKS)]
+        ex = [keep.tile([P, D, P], F32, name="ex%d" % b) for b in range(BLOCKS)]
+        th = [keep.tile([P, D, P], F32, name="th%d" % b) for b in range(BLOCKS)]
+        top = [keep.tile([P, P], F32, name="top%d" % b) for b in range(BLOCKS)]
+        shift = [keep.tile([P, P], F32, name="shift%d" % b, tag="shift%d" % b) for b in range(BLOCKS)]
+
+        def largest(b):
             nc.vector.tensor_reduce(
-                out=top[:], in_=y_ps[:].rearrange("p d t -> p t d"), axis=mybir.AxisListType.X, op=ALU.max
+                out=top[b][:], in_=y_ps[b][:].rearrange("p d t -> p t d"), axis=mybir.AxisListType.X, op=ALU.max
             )
-            shift = keep.tile([P, P], F32, name="shift%d" % b, tag="shift%d" % b)
-            nc.vector.scalar_tensor_tensor(shift[:], top[:], -REACH, pos_t[:, b, :], ALU.add, ALU.max)
+
+        def choose_shift(b):
+            nc.vector.scalar_tensor_tensor(shift[b][:], top[b][:], -REACH, pos_t[:, b, :], ALU.add, ALU.max)
+
+        def shifted(b):
             nc.vector.tensor_tensor(
-                u[b][:], y_ps[:], shift[:].unsqueeze(1).to_broadcast([P, D, P]), ALU.subtract
+                u[b][:], y_ps[b][:], shift[b][:].unsqueeze(1).to_broadcast([P, D, P]), ALU.subtract
             )
             nc.scalar.activation(out=ex[b][:], in_=u[b][:], func=ACT.Exp)
             nc.scalar.activation(out=th[b][:], in_=u[b][:], func=ACT.Tanh, scale=-0.5)
@@ -160,34 +175,47 @@ def tile_picked_ytop1_bpr_p_kernel(
                 ALU.add,
                 ALU.mult,
             )
-            add_turned(sum_wt[:, b, :], wt)
+            add_turned(sum_wt[b // last][:, b % last, :], wt)
 
         hidden(0)
         hidden(1)
-        pos_t = psum.tile([P, BLOCKS, P], F32, name="pos_t", tag="ha")
+        pos_t = psum.tile([P, BLOCKS, P], F32, name="pos_t", tag="sw")
         for b in range(BLOCKS):
             nc.tensor.transpose(pos_t[:, b, :], pos_sb[:, b, :], ident[:])
+        hidden(2)
+        scores(0)
+        hidden(3)
+        scores(1)
+        largest(0)
+        choose_shift(0)
+        for b in range(1, BLOCKS):
+            largest(b)
+            if b == 1:
+                scores(2)
+            shifted(b - 1)
+            choose_shift(b)
+            if b == 1:
+                scores(3)
+        shifted(BLOCKS - 1)
+        last = BLOCKS - 1
+        pieces = [slice(0, last), slice(last, BLOCKS)]
+        sum_ex = [psum.tile([P, last, V], F32, name="sum_ex0", tag="se"), psum.tile([P, 1, V], F32, name="sum_ex1", tag="ya")]
+        sum_wt = [psum.tile([P, last, V], F32, name="sum_wt0", tag="sw"), psum.tile([P, 1, V], F32, name="sum_wt1", tag="hb")]
         for b in range(BLOCKS):
-            scores(b)
-            if b + 2 < BLOCKS:
-                hidden(b + 2)
-            if b >= 1:
-                add_turned(sum_ex[:, b - 1, :], ex[b - 1])
-        add_turned(sum_ex[:, BLOCKS - 1, :], ex[BLOCKS - 1])
+            add_turned(sum_ex[b // last][:, b % last, :], ex[b])
         wt_all = keep.tile([P, BLOCKS, D, P], F32, name="wt_all", tag="shift%d" % (BLOCKS - 1))
         for b in range(BLOCKS):
             weigh(b)
 
         out_rows = out.rearrange("(b p) v -> p b v", p=P)
         log_ex = u[BLOCKS - 1]
-        nc.scalar.activation(out=log_ex[:], in_=sum_ex[:], func=ACT.Ln, bias=FLOOR)
         log_wt = u[BLOCKS - 2]
-        for a in range(2):
-            pair = slice(2 * a, 2 * a + 2)
+        for a, pair in enumerate(pieces):
+            nc.scalar.activation(out=log_ex[:, pair, :], in_=sum_ex[a][:], func=ACT.Ln, bias=FLOOR)
             nc.scalar.activation(
-                out=log_wt[:, pair, :], in_=sum_wt[:, pair, :], func=ACT.Ln, scale=0.5 / (1.0 + EPS), bias=FLOOR
+                out=log_wt[:, pair, :], in_=sum_wt[a][:], func=ACT.Ln, scale=0.5 / (1.0 + EPS), bias=FLOOR
             )
-            res = keep.tile([P, 2, V], F32, name="res%d" % a)
+            res = keep.tile([P, pair.stop - pair.start, V], F32, name="res%d" % a)
             nc.vector.scalar_tensor_tensor(
                 res[:], log_ex[:, pair, :], -math.log(1.0 + EPS), log_wt[:, pair, :], ALU.add, ALU.subtract
             )

@@ -20,16 +20,19 @@ ACT = mybir.ActivationFunctionType
 P = 128
 PACK = 4
 BLOCKS = S // P
-REACH = 32.0
+REACH = 24.0
+KNEE = 32.0
 EPS = 1e-3
-FLOOR = 2.0**-50
-M_SCALAR = 64
+CUTS = 2
+W_CUTS = [(0, 128), (128, 320), (320, 512)]
+POS_AT = 4 * W
+W_AT = POS_AT + 4 * S
 
 
-def load_scale_rows(engines, plane, scales):
-    rows = scales[0].rearrange("(q r) c -> r q c", r=4)
-    for r, engine in enumerate(engines):
-        engine.dma_start(out=plane[r:P:32, :].bitcast(I32), in_=rows[r].bitcast(I32))
+def place_scale_rows(engine, plane):
+    words = plane[:].bitcast(I32)
+    for r in range(1, 4):
+        engine.dma_start(out=words[r:P:32, :], in_=words[8 * r : P : 32, :])
 
 
 def tile_picked_ytop1_bpr_p_kernel(
@@ -39,75 +42,76 @@ def tile_picked_ytop1_bpr_p_kernel(
     with ExitStack() as ctx:
         keep = ctx.enter_context(tc.tile_pool(name="keep", bufs=1))
         psum = ctx.enter_context(tc.psum_pool(name="psum", bufs=1))
+        late = ctx.enter_context(tc.tile_pool(name="late", bufs=1))
 
         offs_t = keep.tile([P, S // 16], U16, name="offs_t")
         neg_t = keep.tile([P, U // 16], U16, name="neg_t")
-        w_raw = keep.tile([P, PACK, H], F32, name="w_raw")
+        w_raw = [keep.tile([P, PACK, b - a], F32, name="w_raw%d" % a) for a, b in W_CUTS]
         x_tab = keep.tile([P, T], U32, name="x_tab", align_bytes=64)
-        xs_tab = keep.tile([P, T], U8, name="xs_tab", tag="xs", align_bytes=64)
-        e_tab = keep.tile([P, W], U32, name="e_tab", tag="h_q0", align_bytes=64)
-        es_tab = keep.tile([P, W], U8, name="es_tab", tag="es", align_bytes=64)
+        e_tab = late.tile([P, W], U32, name="e_tab", offset=0, align_bytes=64)
+        xs_tab = keep.tile([P, T], U8, name="xs_tab", align_bytes=64)
+        es_tab = keep.tile([P, W], U8, name="es_tab", align_bytes=64)
         ident = keep.tile([P, P], F32, name="ident")
+        zero = keep.tile([P, 1], F32, name="zero")
 
-        pos_sb = keep.tile([P, BLOCKS, V], F32, name="pos_sb")
-        for plane in (es_tab, xs_tab):
+        for plane in (xs_tab, es_tab):
             words = plane[:].bitcast(I32)
-            mid = words.shape[1] // 2
-            nc.gpsimd.memset(words[:, :mid], 0)
-            nc.vector.memset(words[:, mid:], 0)
-        nc.sync.dma_start(neg_t[:], neg)
+            nc.gpsimd.memset(words[:, :P], 0)
+            nc.vector.memset(words[:, P:], 0)
+        nc.vector.memset(zero[:], 0.0)
+        half_one = keep.tile([P, 1], F32, name="half_one")
+        nc.scalar.activation(out=half_one[:], in_=zero[:], func=ACT.Sigmoid)
+        w_rows = w1.rearrange("(p j) c -> p j c", j=PACK)
         nc.sync.dma_start(offs_t[:], offs)
-        load_scale_rows([nc.sync] * 4, es_tab, e_scales)
-        nc.sync.dma_start(out=w_raw[:], in_=w1.rearrange("(p j) c -> p j c", j=PACK))
-        load_scale_rows([nc.sync] * 4, xs_tab, x_scales)
+        nc.sync.dma_start(neg_t[:], neg)
+        nc.sync.dma_start(out=w_raw[0][:], in_=w_rows[:, :, : W_CUTS[0][1]])
+        nc.sync.dma_start(out=xs_tab[0:P:8, :].bitcast(I32), in_=x_scales[0].bitcast(I32))
+        nc.sync.dma_start(out=es_tab[0:P:8, :].bitcast(I32), in_=e_scales[0].bitcast(I32))
+        for i in (1, 2):
+            nc.sync.dma_start(out=w_raw[i][:], in_=w_rows[:, :, W_CUTS[i][0] : W_CUTS[i][1]])
         nc.sync.dma_start(out=x_tab[:].bitcast(I32), in_=x_words[0].rearrange("p n t -> p (n t)").bitcast(I32))
         nc.sync.dma_start(out=e_tab[:].bitcast(I32), in_=e_words[0].rearrange("p n t -> p (n t)").bitcast(I32))
-        nc.sync.dma_start(out=pos_sb[:], in_=pos.rearrange("(b p) v -> p b v", p=P))
         make_identity(nc, ident[:])
 
-        e_sc_list = keep.tile([P, U], U8, name="e_sc_list", align_bytes=64)
-        nc.vector.tensor_copy(e_sc_list[:], es_tab[:].indirect(neg_t[:]))
-        e_sc = keep.tile([P, U], U8, name="e_sc", align_bytes=64)
-        nc.vector.tensor_copy(
-            out=e_sc[:].rearrange("p (d v) -> p d v", d=D),
-            in_=e_sc_list[:].rearrange("p (v d) -> p d v", d=D),
-        )
-        w_bf = keep.tile([P, PACK * H], BF16, name="w_bf", align_bytes=64)
+        x_sc_list = keep.tile([P, S], U8, name="x_sc_list", align_bytes=64)
+        nc.vector.tensor_copy(x_sc_list[:], xs_tab[:].indirect(offs_t[:]))
+        x_sc = keep.tile([P, S], U8, name="x_sc", align_bytes=64)
+        nc.vector.tensor_copy(x_sc[:].bitcast(I32), x_sc_list[:].bitcast(I32))
+        place_scale_rows(nc.sync, x_sc)
+
+        w_bf = late.tile([P, PACK * H], BF16, name="w_bf", offset=W_AT, align_bytes=64)
         w_dst = w_bf[:].rearrange("p (t m j) -> p m t j", t=PACK, j=PACK)
-        w_src = w_raw[:].rearrange("p j (m t) -> p m t j", t=PACK)
-        nc.scalar.activation(out=w_dst[:, :M_SCALAR], in_=w_src[:, :M_SCALAR], func=ACT.Copy)
-        nc.vector.tensor_copy(out=w_dst[:, M_SCALAR:], in_=w_src[:, M_SCALAR:])
+        for i, (a, b) in enumerate(W_CUTS):
+            nc.scalar.activation(
+                out=w_dst[:, a // PACK : b // PACK], in_=w_raw[i][:].rearrange("p j (m t) -> p m t j", t=PACK), func=ACT.Copy
+            )
 
-        half = S // 2
-        offs_half = [offs_t[:, a * half // 16 : (a + 1) * half // 16] for a in range(2)]
-        x_sc = [keep.tile([P, half], U8, name="x_sc%d" % a, align_bytes=64) for a in range(2)]
-        nc.vector.tensor_copy(x_sc[0][:], xs_tab[:].indirect(offs_half[0]))
-
+        e_sc_list = late.tile([P, U], U8, name="e_sc_list", offset=POS_AT, align_bytes=64)
+        nc.vector.tensor_copy(e_sc_list[:], es_tab[:].indirect(neg_t[:]))
         w_q = keep.tile([P, H], U32, name="w_q", align_bytes=64)
         w_sc = keep.tile([P, H], U8, name="w_sc", align_bytes=64)
+        e_sc = keep.tile([P, U], U8, name="e_sc", align_bytes=64)
+        nc.vector.tensor_copy(e_sc[:].bitcast(I32), e_sc_list[:].bitcast(I32))
+        place_scale_rows(nc.sync, e_sc)
         nc.vector.quantize_mx(out=w_q[:].bitcast(FP8X4), scales=w_sc[:], in_=w_bf[:])
+        pos_sb = late.tile([P, BLOCKS, V], F32, name="pos_sb", offset=POS_AT, align_bytes=64)
+        nc.sync.dma_start(out=pos_sb[:], in_=pos.rearrange("(b p) v -> p b v", p=P))
 
+        half = S // 2
         x_q = []
 
-        def gather_x(a, tag):
-            words = keep.tile([P, half], U32, name="x_q%d" % a, tag=tag, align_bytes=64)
-            nc.vector.tensor_copy(words[:], x_tab[:].indirect(offs_half[a]))
+        def gather_x(a):
+            words = late.tile([P, half], U32, name="x_q%d" % a, offset=W_AT + 4 * half * a, align_bytes=64)
+            nc.vector.tensor_copy(words[:], x_tab[:].indirect(offs_t[:, a * half // 16 : (a + 1) * half // 16]))
             x_q.append(words)
 
-        nc.vector.tensor_copy(x_sc[1][:], xs_tab[:].indirect(offs_half[1]))
-        gather_x(0, "x_q0")
-        gather_x(1, "x_q1")
-        e_q = keep.tile([P, U], U32, name="e_q", align_bytes=64)
-        nc.vector.tensor_copy(e_q[:].rearrange("p (d v) -> p v d", d=D), e_tab[:].indirect(neg_t[:]))
-
-        h_q = [keep.tile([P, P], U32, name="h_q%d" % b, tag="h_q%d" % b, align_bytes=64) for b in range(BLOCKS)]
+        h_q = [late.tile([P, P], U32, name="h_q%d" % b, offset=4 * P * b, align_bytes=64) for b in range(BLOCKS)]
         h_sc = [keep.tile([P, P], U8, name="h_sc%d" % b, align_bytes=64) for b in range(BLOCKS)]
-
         h_bf = {}
         y_ps = {}
 
         def hidden(b):
-            h_ps = psum.tile([P, PACK, P], F32, name="h_ps%d" % b, tag=["ha", "hb", "hc", "hb"][b])
+            h_ps = psum.tile([P, PACK, P], F32, name="h_ps%d" % b, tag="bank%d" % b)
             cols = slice((b % 2) * P, (b % 2 + 1) * P)
             for t in range(PACK):
                 wc = slice(t * P, (t + 1) * P)
@@ -116,107 +120,100 @@ def tile_picked_ytop1_bpr_p_kernel(
                     lhsT=w_q[:, wc].bitcast(FP8X4),
                     lhsT_scale=w_sc[:, wc],
                     rhs=x_q[b // 2][:, cols].bitcast(FP8X4),
-                    rhs_scale=x_sc[b // 2][:, cols],
+                    rhs_scale=x_sc[:, b * P : (b + 1) * P],
                     start=True,
                     stop=True,
                 )
-            h_bf[b] = keep.tile([P, P, PACK], BF16, name="h_bf%d" % b, tag="h_bf%d" % b, align_bytes=64)
+            h_bf[b] = keep.tile([P, P, PACK], BF16, name="h_bf%d" % b, align_bytes=64)
             nc.scalar.copy(out=h_bf[b][:], in_=h_ps[:].rearrange("p t n -> p n t"))
 
         def scores(b):
             nc.vector.quantize_mx(
                 out=h_q[b][:].bitcast(FP8X4), scales=h_sc[b][:], in_=h_bf[b][:].rearrange("p n t -> p (n t)")
             )
-            y_ps[b] = psum.tile([P, D, P], F32, name="y_ps%d" % b, tag=["ya", "yb", "yc", "hc"][b])
-            for d in range(D):
-                ec = slice(d * P, (d + 1) * P)
-                nc.tensor.matmul_mx(
-                    out=y_ps[b][:, d, :],
-                    lhsT=e_q[:, ec].bitcast(FP8X4),
-                    lhsT_scale=e_sc[:, ec],
-                    rhs=h_q[b][:].bitcast(FP8X4),
-                    rhs_scale=h_sc[b][:],
-                    start=True,
-                    stop=True,
-                )
-
-        u = [keep.tile([P, D, P], F32, name="u%d" % b) for b in range(BLOCKS)]
-        ex = [keep.tile([P, D, P], F32, name="ex%d" % b) for b in range(BLOCKS)]
-        th = [keep.tile([P, D, P], F32, name="th%d" % b) for b in range(BLOCKS)]
-        top = [keep.tile([P, P], F32, name="top%d" % b) for b in range(BLOCKS)]
-        shift = [keep.tile([P, P], F32, name="shift%d" % b, tag="shift%d" % b) for b in range(BLOCKS)]
-
-        def largest(b):
-            nc.vector.tensor_reduce(
-                out=top[b][:], in_=y_ps[b][:].rearrange("p d t -> p t d"), axis=mybir.AxisListType.X, op=ALU.max
+            y_ps[b] = psum.tile([P, V, D], F32, name="y_ps%d" % b, tag="bank%d" % (BLOCKS + b))
+            nc.tensor.matmul_mx(
+                out=y_ps[b][:].rearrange("p v d -> p (v d)"),
+                lhsT=h_q[b][:].bitcast(FP8X4),
+                lhsT_scale=h_sc[b][:],
+                rhs=e_q[:].bitcast(FP8X4),
+                rhs_scale=e_sc[:],
+                start=True,
+                stop=True,
             )
 
-        def choose_shift(b):
-            nc.vector.scalar_tensor_tensor(shift[b][:], top[b][:], -REACH, pos_t[:, b, :], ALU.add, ALU.max)
+        last = BLOCKS - 1
+        u = [keep.tile([P, D, V // CUTS], F32, name="u%d" % i) for i in range(BLOCKS * CUTS)]
+        ex = [keep.tile([P, D, V], F32, name="ex%d" % b) for b in range(BLOCKS)]
+        sg = [keep.tile([P, D, V], F32, name="sg%d" % b) for b in range(BLOCKS)]
+        parts = [(b, slice(a * V // CUTS, (a + 1) * V // CUTS)) for b in range(BLOCKS) for a in range(CUTS)]
+        width = V // CUTS
+        top = [keep.tile([P, width], F32, name="top%d" % i) for i in range(len(parts))]
+        shift = [keep.tile([P, width], F32, name="shift%d" % i) for i in range(len(parts))]
 
-        def shifted(b):
+        def largest(i):
+            b, vs = parts[i]
+            nc.vector.tensor_reduce(out=top[i][:], in_=y_ps[b][:, vs, :], axis=mybir.AxisListType.X, op=ALU.max)
+
+        def choose_shift(i):
+            b, vs = parts[i]
+            nc.vector.scalar_tensor_tensor(shift[i][:], top[i][:], REACH, pos_sb[:, b, vs], ALU.add, ALU.min)
+
+        def shifted(i):
+            b, vs = parts[i]
             nc.vector.tensor_tensor(
-                u[b][:], y_ps[b][:], shift[b][:].unsqueeze(1).to_broadcast([P, D, P]), ALU.subtract
+                u[i][:],
+                y_ps[b][:, vs, :].rearrange("p v d -> p d v"),
+                shift[i][:].unsqueeze(1).to_broadcast([P, D, width]),
+                ALU.subtract,
             )
-            nc.scalar.activation(out=ex[b][:], in_=u[b][:], func=ACT.Exp)
-            nc.scalar.activation(out=th[b][:], in_=u[b][:], func=ACT.Tanh, scale=-0.5)
+            nc.scalar.activation(out=ex[b][:, :, vs], in_=u[i][:], func=ACT.Sigmoid, bias=-KNEE)
+            nc.scalar.activation(out=sg[b][:, :, vs], in_=u[i][:], func=ACT.Sigmoid)
 
-        def add_turned(dst, src):
-            for d in range(D):
+        def add_turned(dst, src, ds):
+            for d in ds:
                 nc.tensor.matmul(dst, src[:, d, :], ident[:], start=(d == 0), stop=(d == D - 1), is_transpose=True)
 
-        def weigh(b):
-            wt = wt_all[:, b]
-            nc.vector.scalar_tensor_tensor(
-                wt.rearrange("p d t -> p (d t)"),
-                th[b][:].rearrange("p d t -> p (d t)"),
-                1.0 + 2.0 * EPS,
-                ex[b][:].rearrange("p d t -> p (d t)"),
-                ALU.add,
-                ALU.mult,
-            )
-            add_turned(sum_wt[b // last][:, b % last, :], wt)
-
-        hidden(0)
-        hidden(1)
-        pos_t = psum.tile([P, BLOCKS, P], F32, name="pos_t", tag="sw")
+        gather_x(0)
+        gather_x(1)
+        e_q = late.tile([P, U], U32, name="e_q", offset=W_AT + 4 * S, align_bytes=64)
+        nc.vector.tensor_copy(e_q[:], e_tab[:].indirect(neg_t[:]))
         for b in range(BLOCKS):
-            nc.tensor.transpose(pos_t[:, b, :], pos_sb[:, b, :], ident[:])
-        hidden(2)
-        scores(0)
-        hidden(3)
-        scores(1)
+            hidden(b)
+        for b in range(BLOCKS):
+            scores(b)
         largest(0)
         choose_shift(0)
-        for b in range(1, BLOCKS):
-            largest(b)
-            if b == 1:
-                scores(2)
-            shifted(b - 1)
-            choose_shift(b)
-            if b == 1:
-                scores(3)
-        shifted(BLOCKS - 1)
-        last = BLOCKS - 1
-        pieces = [slice(0, last), slice(last, BLOCKS)]
-        sum_ex = [psum.tile([P, last, V], F32, name="sum_ex0", tag="se"), psum.tile([P, 1, V], F32, name="sum_ex1", tag="ya")]
-        sum_wt = [psum.tile([P, last, V], F32, name="sum_wt0", tag="sw"), psum.tile([P, 1, V], F32, name="sum_wt1", tag="hb")]
-        for b in range(BLOCKS):
-            add_turned(sum_ex[b // last][:, b % last, :], ex[b])
-        wt_all = keep.tile([P, BLOCKS, D, P], F32, name="wt_all", tag="shift%d" % (BLOCKS - 1))
-        for b in range(BLOCKS):
-            weigh(b)
+        for i in range(1, len(parts)):
+            largest(i)
+            shifted(i - 1)
+            choose_shift(i)
+        shifted(len(parts) - 1)
 
-        out_rows = out.rearrange("(b p) v -> p b v", p=P)
-        log_ex = u[BLOCKS - 1]
-        log_wt = u[BLOCKS - 2]
-        for a, pair in enumerate(pieces):
-            nc.scalar.activation(out=log_ex[:, pair, :], in_=sum_ex[a][:], func=ACT.Ln, bias=FLOOR)
-            nc.scalar.activation(
-                out=log_wt[:, pair, :], in_=sum_wt[a][:], func=ACT.Ln, scale=0.5 / (1.0 + EPS), bias=FLOOR
+        pieces = [range(0, last), range(last, BLOCKS)]
+        sum_ex = [psum.tile([P, len(pieces[a]), P], F32, name="sum_ex%d" % a, tag="bank%d" % (2 * a)) for a in range(2)]
+        sum_sg = [psum.tile([P, len(pieces[a]), P], F32, name="sum_sg%d" % a, tag="bank%d" % (2 * a + 1)) for a in range(2)]
+        for b in range(last):
+            add_turned(sum_ex[0][:, b, :], ex[b], range(D))
+            add_turned(sum_sg[0][:, b, :], sg[b], range(D))
+        add_turned(sum_ex[1][:, 0, :], ex[last], range(D))
+        add_turned(sum_sg[1][:, 0, :], sg[last], range(D))
+
+        back = []
+        for a, piece in enumerate(pieces):
+            n = len(piece)
+            both = keep.tile([P, 2, n, P], F32, name="both%d" % a)
+            nc.vector.tensor_scalar(
+                both[:, 0], sum_ex[a][:], half_one[:], 2.0 * EPS * math.exp(KNEE), ALU.mult, ALU.mult
             )
-            res = keep.tile([P, pair.stop - pair.start, V], F32, name="res%d" % a)
-            nc.vector.scalar_tensor_tensor(
-                res[:], log_ex[:, pair, :], -math.log(1.0 + EPS), log_wt[:, pair, :], ALU.add, ALU.subtract
-            )
-            nc.sync.dma_start(out=out_rows[:, pair, :], in_=res[:])
+            nc.vector.tensor_tensor(both[:, 1], sum_sg[a][:], both[:, 0], ALU.add)
+            for b in piece:
+                back.append(psum.tile([P, 2, V], F32, name="back%d" % b, tag="bank%d" % (BLOCKS + b)))
+                for i in range(2):
+                    nc.tensor.transpose(back[b][:, i, :], both[:, i, b - piece.start, :], ident[:])
+        for b in range(BLOCKS):
+            logs = keep.tile([P, 2, V], F32, name="logs%d" % b)
+            nc.scalar.activation(out=logs[:], in_=back[b][:], func=ACT.Ln)
+            res = keep.tile([P, V], F32, name="res%d" % b)
+            nc.vector.scalar_tensor_tensor(res[:], logs[:, 0], -math.log(EPS), logs[:, 1], ALU.add, ALU.subtract)
+            nc.sync.dma_start(out=out[b * P : (b + 1) * P, :], in_=res[:])

@@ -23,7 +23,6 @@ BLOCKS = S // P
 REACH = 24.0
 KNEE = 32.0
 EPS = 1e-3
-CUTS = 2
 W_CUTS = [(0, 128), (128, 320), (320, 512)]
 POS_AT = 4 * W
 W_AT = POS_AT + 4 * S
@@ -70,14 +69,14 @@ def tile_picked_ytop1_bpr_p_kernel(
         for i in (1, 2):
             nc.sync.dma_start(out=w_raw[i][:], in_=w_rows[:, :, W_CUTS[i][0] : W_CUTS[i][1]])
         nc.sync.dma_start(out=x_tab[:].bitcast(I32), in_=x_words[0].rearrange("p n t -> p (n t)").bitcast(I32))
-        nc.sync.dma_start(out=e_tab[:].bitcast(I32), in_=e_words[0].rearrange("p n t -> p (n t)").bitcast(I32))
         make_identity(nc, ident[:])
 
-        x_sc_list = keep.tile([P, S], U8, name="x_sc_list", align_bytes=64)
+        x_sc_list = late.tile([P, S], U8, name="x_sc_list", offset=0, align_bytes=64)
         nc.vector.tensor_copy(x_sc_list[:], xs_tab[:].indirect(offs_t[:]))
         x_sc = keep.tile([P, S], U8, name="x_sc", align_bytes=64)
         nc.vector.tensor_copy(x_sc[:].bitcast(I32), x_sc_list[:].bitcast(I32))
         place_scale_rows(nc.sync, x_sc)
+        nc.sync.dma_start(out=e_tab[:].bitcast(I32), in_=e_words[0].rearrange("p n t -> p (n t)").bitcast(I32))
 
         w_bf = late.tile([P, PACK * H], BF16, name="w_bf", offset=W_AT, align_bytes=64)
         w_dst = w_bf[:].rearrange("p (t m j) -> p m t j", t=PACK, j=PACK)
@@ -131,29 +130,39 @@ def tile_picked_ytop1_bpr_p_kernel(
             nc.vector.quantize_mx(
                 out=h_q[b][:].bitcast(FP8X4), scales=h_sc[b][:], in_=h_bf[b][:].rearrange("p n t -> p (n t)")
             )
-            y_ps[b] = psum.tile([P, V, D], F32, name="y_ps%d" % b, tag="bank%d" % (BLOCKS + b))
-            nc.tensor.matmul_mx(
-                out=y_ps[b][:].rearrange("p v d -> p (v d)"),
-                lhsT=h_q[b][:].bitcast(FP8X4),
-                lhsT_scale=h_sc[b][:],
-                rhs=e_q[:].bitcast(FP8X4),
-                rhs_scale=e_sc[:],
-                start=True,
-                stop=True,
-            )
+            cuts = 2 if b == 0 else 1
+            for a in range(cuts):
+                n = U // cuts
+                bank = psum.tile([P, n // D, D], F32, name="y_ps%d%d" % (b, a), tag="bank%d" % (BLOCKS + b if a == 0 else 0))
+                nc.tensor.matmul_mx(
+                    out=bank[:].rearrange("p v d -> p (v d)"),
+                    lhsT=h_q[b][:].bitcast(FP8X4),
+                    lhsT_scale=h_sc[b][:],
+                    rhs=e_q[:, a * n : (a + 1) * n].bitcast(FP8X4),
+                    rhs_scale=e_sc[:, a * n : (a + 1) * n],
+                    start=True,
+                    stop=True,
+                )
+                y_ps[b, a] = bank
+
+        def scores_of(i):
+            b, vs = parts[i]
+            if b == 0:
+                return y_ps[b, i][:]
+            return y_ps[b, 0][:, vs, :]
 
         last = BLOCKS - 1
-        u = [keep.tile([P, D, V // CUTS], F32, name="u%d" % i) for i in range(BLOCKS * CUTS)]
+        parts = [(b, slice(a * V // 2, (a + 1) * V // 2)) for b in range(BLOCKS) for a in range(2)][:-1]
+        parts += [(last, slice(a * V // 4, (a + 1) * V // 4)) for a in (2, 3)]
+        u = [keep.tile([P, D, vs.stop - vs.start], F32, name="u%d" % i) for i, (b, vs) in enumerate(parts)]
         ex = [keep.tile([P, D, V], F32, name="ex%d" % b) for b in range(BLOCKS)]
         sg = [keep.tile([P, D, V], F32, name="sg%d" % b) for b in range(BLOCKS)]
-        parts = [(b, slice(a * V // CUTS, (a + 1) * V // CUTS)) for b in range(BLOCKS) for a in range(CUTS)]
-        width = V // CUTS
-        top = [keep.tile([P, width], F32, name="top%d" % i) for i in range(len(parts))]
-        shift = [keep.tile([P, width], F32, name="shift%d" % i) for i in range(len(parts))]
+        top = [late.tile([P, V // 2], F32, name="top0", offset=4 * P * last - V, align_bytes=64)]
+        top.extend([keep.tile([P, vs.stop - vs.start], F32, name="top%d" % (i + 1)) for i, (b, vs) in enumerate(parts[1:])])
+        shift = [keep.tile([P, vs.stop - vs.start], F32, name="shift%d" % i) for i, (b, vs) in enumerate(parts)]
 
         def largest(i):
-            b, vs = parts[i]
-            nc.vector.tensor_reduce(out=top[i][:], in_=y_ps[b][:, vs, :], axis=mybir.AxisListType.X, op=ALU.max)
+            nc.vector.tensor_reduce(out=top[i][:], in_=scores_of(i), axis=mybir.AxisListType.X, op=ALU.max)
 
         def choose_shift(i):
             b, vs = parts[i]
@@ -163,8 +172,8 @@ def tile_picked_ytop1_bpr_p_kernel(
             b, vs = parts[i]
             nc.vector.tensor_tensor(
                 u[i][:],
-                y_ps[b][:, vs, :].rearrange("p v d -> p d v"),
-                shift[i][:].unsqueeze(1).to_broadcast([P, D, width]),
+                scores_of(i).rearrange("p v d -> p d v"),
+                shift[i][:].unsqueeze(1).to_broadcast([P, D, vs.stop - vs.start]),
                 ALU.subtract,
             )
             nc.scalar.activation(out=ex[b][:, :, vs], in_=u[i][:], func=ACT.Sigmoid, bias=-KNEE)
@@ -180,10 +189,12 @@ def tile_picked_ytop1_bpr_p_kernel(
         nc.vector.tensor_copy(e_q[:], e_tab[:].indirect(neg_t[:]))
         for b in range(BLOCKS):
             hidden(b)
-        for b in range(BLOCKS):
-            scores(b)
+        scores(0)
+        scores(1)
         largest(0)
         choose_shift(0)
+        scores(2)
+        scores(3)
         for i in range(1, len(parts)):
             largest(i)
             shifted(i - 1)

@@ -24,8 +24,8 @@ REACH = 24.0
 KNEE = 32.0
 EPS = 1e-3
 W_CUTS = [(0, 128), (128, 320), (320, 512)]
-POS_AT = 4 * W
-W_AT = POS_AT + 4 * S
+W_AT = 4 * W
+POS_AT = W_AT + 2 * PACK * H
 
 
 def place_scale_rows(engine, plane):
@@ -71,37 +71,47 @@ def tile_picked_ytop1_bpr_p_kernel(
         nc.sync.dma_start(out=x_tab[:].bitcast(I32), in_=x_words[0].rearrange("p n t -> p (n t)").bitcast(I32))
         make_identity(nc, ident[:])
 
-        x_sc_list = late.tile([P, S], U8, name="x_sc_list", offset=0, align_bytes=64)
-        nc.vector.tensor_copy(x_sc_list[:], xs_tab[:].indirect(offs_t[:]))
-        x_sc = keep.tile([P, S], U8, name="x_sc", align_bytes=64)
-        nc.vector.tensor_copy(x_sc[:].bitcast(I32), x_sc_list[:].bitcast(I32))
-        place_scale_rows(nc.sync, x_sc)
-        nc.sync.dma_start(out=e_tab[:].bitcast(I32), in_=e_words[0].rearrange("p n t -> p (n t)").bitcast(I32))
+        half = S // 2
+        offs_half = [offs_t[:, a * half // 16 : (a + 1) * half // 16] for a in range(2)]
+        x_sc_list = [
+            late.tile([P, half], U8, name="x_sc_list0", offset=0, align_bytes=64),
+            keep.tile([P, half], U8, name="x_sc_list1", align_bytes=64),
+        ]
+        x_sc = [keep.tile([P, half], U8, name="x_sc%d" % a, align_bytes=64) for a in range(2)]
 
-        w_bf = late.tile([P, PACK * H], BF16, name="w_bf", offset=W_AT, align_bytes=64)
-        w_dst = w_bf[:].rearrange("p (t m j) -> p m t j", t=PACK, j=PACK)
+        def place_x_scales(a):
+            nc.vector.tensor_copy(x_sc[a][:].bitcast(I32), x_sc_list[a][:].bitcast(I32))
+            place_scale_rows(nc.sync, x_sc[a])
+
+        nc.vector.tensor_copy(x_sc_list[0][:], xs_tab[:].indirect(offs_half[0]))
+        place_x_scales(0)
+        nc.sync.dma_start(out=e_tab[:].bitcast(I32), in_=e_words[0].rearrange("p n t -> p (n t)").bitcast(I32))
+        nc.vector.tensor_copy(x_sc_list[1][:], xs_tab[:].indirect(offs_half[1]))
+
+        w_bf = late.tile([P, PACK * H + 32], BF16, name="w_bf", offset=W_AT, align_bytes=64)
+        w_dst = w_bf[:, : PACK * H].rearrange("p (t m j) -> p m t j", t=PACK, j=PACK)
         for i, (a, b) in enumerate(W_CUTS):
             nc.scalar.activation(
                 out=w_dst[:, a // PACK : b // PACK], in_=w_raw[i][:].rearrange("p j (m t) -> p m t j", t=PACK), func=ACT.Copy
             )
 
-        e_sc_list = late.tile([P, U], U8, name="e_sc_list", offset=POS_AT, align_bytes=64)
+        e_sc_list = keep.tile([P, U], U8, name="e_sc_list", align_bytes=64)
         nc.vector.tensor_copy(e_sc_list[:], es_tab[:].indirect(neg_t[:]))
+        place_x_scales(1)
         w_q = keep.tile([P, H], U32, name="w_q", align_bytes=64)
         w_sc = keep.tile([P, H], U8, name="w_sc", align_bytes=64)
         e_sc = keep.tile([P, U], U8, name="e_sc", align_bytes=64)
         nc.vector.tensor_copy(e_sc[:].bitcast(I32), e_sc_list[:].bitcast(I32))
         place_scale_rows(nc.sync, e_sc)
-        nc.vector.quantize_mx(out=w_q[:].bitcast(FP8X4), scales=w_sc[:], in_=w_bf[:])
+        nc.vector.quantize_mx(out=w_q[:].bitcast(FP8X4), scales=w_sc[:], in_=w_bf[:, : PACK * H])
         pos_sb = late.tile([P, BLOCKS, V], F32, name="pos_sb", offset=POS_AT, align_bytes=64)
         nc.sync.dma_start(out=pos_sb[:], in_=pos.rearrange("(b p) v -> p b v", p=P))
 
-        half = S // 2
         x_q = []
 
         def gather_x(a):
             words = late.tile([P, half], U32, name="x_q%d" % a, offset=W_AT + 4 * half * a, align_bytes=64)
-            nc.vector.tensor_copy(words[:], x_tab[:].indirect(offs_t[:, a * half // 16 : (a + 1) * half // 16]))
+            nc.vector.tensor_copy(words[:], x_tab[:].indirect(offs_half[a]))
             x_q.append(words)
 
         h_q = [late.tile([P, P], U32, name="h_q%d" % b, offset=4 * P * b, align_bytes=64) for b in range(BLOCKS)]
@@ -119,7 +129,7 @@ def tile_picked_ytop1_bpr_p_kernel(
                     lhsT=w_q[:, wc].bitcast(FP8X4),
                     lhsT_scale=w_sc[:, wc],
                     rhs=x_q[b // 2][:, cols].bitcast(FP8X4),
-                    rhs_scale=x_sc[:, b * P : (b + 1) * P],
+                    rhs_scale=x_sc[b // 2][:, cols],
                     start=True,
                     stop=True,
                 )
@@ -148,16 +158,17 @@ def tile_picked_ytop1_bpr_p_kernel(
         def scores_of(i):
             b, vs = parts[i]
             if b == 0:
-                return y_ps[b, i][:]
+                a = vs.start // (V // 2)
+                return y_ps[b, a][:, vs.start - a * V // 2 : vs.stop - a * V // 2, :]
             return y_ps[b, 0][:, vs, :]
 
         last = BLOCKS - 1
-        parts = [(b, slice(a * V // 2, (a + 1) * V // 2)) for b in range(BLOCKS) for a in range(2)][:-1]
-        parts += [(last, slice(a * V // 4, (a + 1) * V // 4)) for a in (2, 3)]
+        cuts = [[0, 32, 64, V], [0, 64, V], [0, 64, V], [0, 32, 64, 96, V]]
+        parts = [(b, slice(c[i], c[i + 1])) for b, c in enumerate(cuts) for i in range(len(c) - 1)]
         u = [keep.tile([P, D, vs.stop - vs.start], F32, name="u%d" % i) for i, (b, vs) in enumerate(parts)]
         ex = [keep.tile([P, D, V], F32, name="ex%d" % b) for b in range(BLOCKS)]
         sg = [keep.tile([P, D, V], F32, name="sg%d" % b) for b in range(BLOCKS)]
-        top = [late.tile([P, V // 2], F32, name="top0", offset=4 * P * last - V, align_bytes=64)]
+        top = [late.tile([P, V // 4], F32, name="top0", offset=4 * P * last - 64, align_bytes=64)]
         top.extend([keep.tile([P, vs.stop - vs.start], F32, name="top%d" % (i + 1)) for i, (b, vs) in enumerate(parts[1:])])
         shift = [keep.tile([P, vs.stop - vs.start], F32, name="shift%d" % i) for i, (b, vs) in enumerate(parts)]
 

@@ -221,18 +221,25 @@ def tile_picked_ytop1_bpr_p_kernel(
         add_turned(sum_ex[1][:, 0, :], ex[last], range(D))
         add_turned(sum_sg[1][:, 0, :], sg[last], range(D))
 
+        both = [keep.tile([P, 2, P], F32, name="both%d" % b) for b in range(BLOCKS)]
         back = []
-        for a, piece in enumerate(pieces):
-            n = len(piece)
-            both = keep.tile([P, 2, n, P], F32, name="both%d" % a)
+
+        def scale_total(b):
             nc.vector.tensor_scalar(
-                both[:, 0], sum_ex[a][:], half_one[:], 2.0 * EPS * math.exp(KNEE), ALU.mult, ALU.mult
+                both[b][:, 0], sum_ex[b // last][:, b % last, :], half_one[:], 2.0 * EPS * math.exp(KNEE), ALU.mult, ALU.mult
             )
-            nc.vector.tensor_tensor(both[:, 1], sum_sg[a][:], both[:, 0], ALU.add)
-            for b in piece:
-                back.append(psum.tile([P, 2, V], F32, name="back%d" % b, tag="bank%d" % (BLOCKS + b)))
-                for i in range(2):
-                    nc.tensor.transpose(back[b][:, i, :], both[:, i, b - piece.start, :], ident[:])
+
+        def add_total(b):
+            nc.vector.tensor_tensor(both[b][:, 1], sum_sg[b // last][:, b % last, :], both[b][:, 0], ALU.add)
+            back.append(psum.tile([P, 2, V], F32, name="back%d" % b, tag="bank%d" % (BLOCKS + b)))
+            for i in range(2):
+                nc.tensor.transpose(back[b][:, i, :], both[b][:, i, :], ident[:])
+
+        scale_total(0)
+        for b in range(1, BLOCKS):
+            scale_total(b)
+            add_total(b - 1)
+        add_total(last)
         for b in range(BLOCKS):
             logs = keep.tile([P, 2, V], F32, name="logs%d" % b)
             nc.scalar.activation(out=logs[:], in_=back[b][:], func=ACT.Ln)

@@ -28,10 +28,14 @@ W_AT = 4 * W
 POS_AT = W_AT + 2 * PACK * H
 
 
-def place_scale_rows(engine, plane):
-    words = plane[:].bitcast(I32)
-    for r in range(1, 4):
-        engine.dma_start(out=words[r:P:32, :], in_=words[8 * r : P : 32, :])
+ROWS_AT = P - 16
+
+
+def place_scale_rows(engine, plane, picked):
+    dst = plane[:].bitcast(I32)
+    src = picked[:].bitcast(I32)
+    for q in range(4):
+        engine.dma_start(out=dst[32 * q : 32 * q + 4, :], in_=src[ROWS_AT + 4 * q : ROWS_AT + 4 * q + 4, :])
 
 
 def tile_picked_ytop1_bpr_p_kernel(
@@ -48,24 +52,26 @@ def tile_picked_ytop1_bpr_p_kernel(
         w_raw = [keep.tile([P, PACK, b - a], F32, name="w_raw%d" % a) for a, b in W_CUTS]
         x_tab = keep.tile([P, T], U32, name="x_tab", align_bytes=64)
         e_tab = late.tile([P, W], U32, name="e_tab", offset=0, align_bytes=64)
-        xs_tab = keep.tile([P, T], U8, name="xs_tab", align_bytes=64)
+        xs_tab = late.tile([P, T], U8, name="xs_tab", offset=0, align_bytes=64)
         es_tab = keep.tile([P, W], U8, name="es_tab", align_bytes=64)
         ident = keep.tile([P, P], F32, name="ident")
         zero = keep.tile([P, 1], F32, name="zero")
 
-        for plane in (xs_tab, es_tab):
-            words = plane[:].bitcast(I32)
-            nc.gpsimd.memset(words[:, :P], 0)
-            nc.vector.memset(words[:, P:], 0)
+        x_sc = keep.tile([P, S], U8, name="x_sc", align_bytes=64)
+        e_sc = keep.tile([P, U], U8, name="e_sc", align_bytes=64)
         nc.vector.memset(zero[:], 0.0)
+        for table in (xs_tab, es_tab):
+            nc.vector.memset(table[:].bitcast(I32)[:ROWS_AT, :], 0)
+        for plane in (x_sc, e_sc):
+            nc.vector.memset(plane[:].bitcast(I32), 0)
         half_one = keep.tile([P, 1], F32, name="half_one")
         nc.scalar.activation(out=half_one[:], in_=zero[:], func=ACT.Sigmoid)
         w_rows = w1.rearrange("(p j) c -> p j c", j=PACK)
-        nc.sync.dma_start(offs_t[:], offs)
-        nc.sync.dma_start(neg_t[:], neg)
         nc.sync.dma_start(out=w_raw[0][:], in_=w_rows[:, :, : W_CUTS[0][1]])
-        nc.sync.dma_start(out=xs_tab[0:P:8, :].bitcast(I32), in_=x_scales[0].bitcast(I32))
-        nc.sync.dma_start(out=es_tab[0:P:8, :].bitcast(I32), in_=e_scales[0].bitcast(I32))
+        nc.sync.dma_start(offs_t[:], offs)
+        nc.sync.dma_start(out=xs_tab[:].bitcast(I32)[ROWS_AT:, :], in_=x_scales[0].bitcast(I32))
+        nc.sync.dma_start(neg_t[:], neg)
+        nc.sync.dma_start(out=es_tab[:].bitcast(I32)[ROWS_AT:, :], in_=e_scales[0].bitcast(I32))
         for i in (1, 2):
             nc.sync.dma_start(out=w_raw[i][:], in_=w_rows[:, :, W_CUTS[i][0] : W_CUTS[i][1]])
         nc.sync.dma_start(out=x_tab[:].bitcast(I32), in_=x_words[0].rearrange("p n t -> p (n t)").bitcast(I32))
@@ -73,20 +79,10 @@ def tile_picked_ytop1_bpr_p_kernel(
 
         half = S // 2
         offs_half = [offs_t[:, a * half // 16 : (a + 1) * half // 16] for a in range(2)]
-        x_sc_list = [
-            late.tile([P, half], U8, name="x_sc_list0", offset=0, align_bytes=64),
-            keep.tile([P, half], U8, name="x_sc_list1", align_bytes=64),
-        ]
-        x_sc = [keep.tile([P, half], U8, name="x_sc%d" % a, align_bytes=64) for a in range(2)]
-
-        def place_x_scales(a):
-            nc.vector.tensor_copy(x_sc[a][:].bitcast(I32), x_sc_list[a][:].bitcast(I32))
-            place_scale_rows(nc.sync, x_sc[a])
-
-        nc.vector.tensor_copy(x_sc_list[0][:], xs_tab[:].indirect(offs_half[0]))
-        place_x_scales(0)
+        x_sc_list = keep.tile([P, S], U8, name="x_sc_list", align_bytes=64)
+        nc.vector.tensor_copy(x_sc_list[:], xs_tab[:].indirect(offs_t[:]))
+        place_scale_rows(nc.sync, x_sc, x_sc_list)
         nc.sync.dma_start(out=e_tab[:].bitcast(I32), in_=e_words[0].rearrange("p n t -> p (n t)").bitcast(I32))
-        nc.vector.tensor_copy(x_sc_list[1][:], xs_tab[:].indirect(offs_half[1]))
 
         w_bf = late.tile([P, PACK * H + 32], BF16, name="w_bf", offset=W_AT, align_bytes=64)
         w_dst = w_bf[:, : PACK * H].rearrange("p (t m j) -> p m t j", t=PACK, j=PACK)
@@ -97,12 +93,9 @@ def tile_picked_ytop1_bpr_p_kernel(
 
         e_sc_list = keep.tile([P, U], U8, name="e_sc_list", align_bytes=64)
         nc.vector.tensor_copy(e_sc_list[:], es_tab[:].indirect(neg_t[:]))
-        place_x_scales(1)
         w_q = keep.tile([P, H], U32, name="w_q", align_bytes=64)
         w_sc = keep.tile([P, H], U8, name="w_sc", align_bytes=64)
-        e_sc = keep.tile([P, U], U8, name="e_sc", align_bytes=64)
-        nc.vector.tensor_copy(e_sc[:].bitcast(I32), e_sc_list[:].bitcast(I32))
-        place_scale_rows(nc.sync, e_sc)
+        place_scale_rows(nc.sync, e_sc, e_sc_list)
         nc.vector.quantize_mx(out=w_q[:].bitcast(FP8X4), scales=w_sc[:], in_=w_bf[:, : PACK * H])
         pos_sb = late.tile([P, BLOCKS, V], F32, name="pos_sb", offset=POS_AT, align_bytes=64)
         nc.sync.dma_start(out=pos_sb[:], in_=pos.rearrange("(b p) v -> p b v", p=P))
@@ -129,7 +122,7 @@ def tile_picked_ytop1_bpr_p_kernel(
                     lhsT=w_q[:, wc].bitcast(FP8X4),
                     lhsT_scale=w_sc[:, wc],
                     rhs=x_q[b // 2][:, cols].bitcast(FP8X4),
-                    rhs_scale=x_sc[b // 2][:, cols],
+                    rhs_scale=x_sc[:, b * P : (b + 1) * P],
                     start=True,
                     stop=True,
                 )
@@ -168,8 +161,12 @@ def tile_picked_ytop1_bpr_p_kernel(
         u = [keep.tile([P, D, vs.stop - vs.start], F32, name="u%d" % i) for i, (b, vs) in enumerate(parts)]
         ex = [keep.tile([P, D, V], F32, name="ex%d" % b) for b in range(BLOCKS)]
         sg = [keep.tile([P, D, V], F32, name="sg%d" % b) for b in range(BLOCKS)]
-        top = [late.tile([P, V // 4], F32, name="top0", offset=4 * P * last - 64, align_bytes=64)]
-        top.extend([keep.tile([P, vs.stop - vs.start], F32, name="top%d" % (i + 1)) for i, (b, vs) in enumerate(parts[1:])])
+        top = []
+        for i, (b, vs) in enumerate(parts):
+            if i == 1:
+                top.append(late.tile([P, vs.stop - vs.start], F32, name="top%d" % i, offset=4 * P * last, align_bytes=64))
+            else:
+                top.append(keep.tile([P, vs.stop - vs.start], F32, name="top%d" % i))
         shift = [keep.tile([P, vs.stop - vs.start], F32, name="shift%d" % i) for i, (b, vs) in enumerate(parts)]
 
         def largest(i):
@@ -202,14 +199,15 @@ def tile_picked_ytop1_bpr_p_kernel(
             hidden(b)
         scores(0)
         scores(1)
+        scores(2)
         largest(0)
         choose_shift(0)
-        scores(2)
-        scores(3)
         for i in range(1, len(parts)):
             largest(i)
             shifted(i - 1)
             choose_shift(i)
+            if i == 1:
+                scores(last)
         shifted(len(parts) - 1)
 
         pieces = [range(0, last), range(last, BLOCKS)]

@@ -24,8 +24,9 @@ REACH = 24.0
 KNEE = 32.0
 EPS = 1e-3
 W_CUTS = [(0, 128), (128, 320), (320, 512)]
-W_AT = 4 * W
-POS_AT = W_AT + 2 * PACK * H
+E_AT = 4 * BLOCKS * V
+XS_AT = E_AT - T // 2
+W_AT = E_AT + 4 * W
 
 
 ROWS_AT = P - 16
@@ -51,8 +52,8 @@ def tile_picked_ytop1_bpr_p_kernel(
         neg_t = keep.tile([P, U // 16], U16, name="neg_t")
         w_raw = [keep.tile([P, PACK, b - a], F32, name="w_raw%d" % a) for a, b in W_CUTS]
         x_tab = keep.tile([P, T], U32, name="x_tab", align_bytes=64)
-        e_tab = late.tile([P, W], U32, name="e_tab", offset=0, align_bytes=64)
-        xs_tab = late.tile([P, T], U8, name="xs_tab", offset=0, align_bytes=64)
+        e_tab = late.tile([P, W], U32, name="e_tab", offset=E_AT, align_bytes=64)
+        xs_tab = late.tile([P, T], U8, name="xs_tab", offset=XS_AT, align_bytes=64)
         es_tab = keep.tile([P, W], U8, name="es_tab", align_bytes=64)
         ident = keep.tile([P, P], F32, name="ident")
         zero = keep.tile([P, 1], F32, name="zero")
@@ -83,12 +84,14 @@ def tile_picked_ytop1_bpr_p_kernel(
         nc.vector.tensor_copy(x_sc_list[:], xs_tab[:].indirect(offs_t[:]))
         place_scale_rows(nc.sync, x_sc, x_sc_list)
         nc.sync.dma_start(out=e_tab[:].bitcast(I32), in_=e_words[0].rearrange("p n t -> p (n t)").bitcast(I32))
+        pos_sb = late.tile([P, BLOCKS, V], F32, name="pos_sb", offset=0, align_bytes=64)
+        nc.sync.dma_start(out=pos_sb[:], in_=pos.rearrange("(b p) v -> p b v", p=P))
 
-        w_bf = late.tile([P, PACK * H + 32], BF16, name="w_bf", offset=W_AT, align_bytes=64)
-        w_dst = w_bf[:, : PACK * H].rearrange("p (t m j) -> p m t j", t=PACK, j=PACK)
+        w_bf = late.tile([P, PACK * H], BF16, name="w_bf", offset=W_AT, align_bytes=64)
+        w_dst = w_bf[:, : PACK * H].rearrange("p (t m j) -> p m j t", t=PACK, j=PACK)
         for i, (a, b) in enumerate(W_CUTS):
             nc.scalar.activation(
-                out=w_dst[:, a // PACK : b // PACK], in_=w_raw[i][:].rearrange("p j (m t) -> p m t j", t=PACK), func=ACT.Copy
+                out=w_dst[:, a // PACK : b // PACK], in_=w_raw[i][:].rearrange("p j (m t) -> p m j t", t=PACK), func=ACT.Copy
             )
 
         e_sc_list = keep.tile([P, U], U8, name="e_sc_list", align_bytes=64)
@@ -97,8 +100,11 @@ def tile_picked_ytop1_bpr_p_kernel(
         w_sc = keep.tile([P, H], U8, name="w_sc", align_bytes=64)
         place_scale_rows(nc.sync, e_sc, e_sc_list)
         nc.vector.quantize_mx(out=w_q[:].bitcast(FP8X4), scales=w_sc[:], in_=w_bf[:, : PACK * H])
-        pos_sb = late.tile([P, BLOCKS, V], F32, name="pos_sb", offset=POS_AT, align_bytes=64)
-        nc.sync.dma_start(out=pos_sb[:], in_=pos.rearrange("(b p) v -> p b v", p=P))
+        warm = psum.tile([P, H], F32, name="warm", tag="bank7")
+        for i in range(2):
+            nc.tensor.matmul_mx(
+                out=warm[:], lhsT=w_q[:, :P].bitcast(FP8X4), lhsT_scale=w_sc[:, :P], rhs=w_q[:].bitcast(FP8X4), rhs_scale=w_sc[:], start=True, stop=True
+            )
 
         x_q = []
 
@@ -107,7 +113,7 @@ def tile_picked_ytop1_bpr_p_kernel(
             nc.vector.tensor_copy(words[:], x_tab[:].indirect(offs_half[a]))
             x_q.append(words)
 
-        h_q = [late.tile([P, P], U32, name="h_q%d" % b, offset=4 * P * b, align_bytes=64) for b in range(BLOCKS)]
+        h_q = [late.tile([P, P], U32, name="h_q%d" % b, offset=E_AT + 4 * P * b, align_bytes=64) for b in range(BLOCKS)]
         h_sc = [keep.tile([P, P], U8, name="h_sc%d" % b, align_bytes=64) for b in range(BLOCKS)]
         h_bf = {}
         y_ps = {}
@@ -133,27 +139,23 @@ def tile_picked_ytop1_bpr_p_kernel(
             nc.vector.quantize_mx(
                 out=h_q[b][:].bitcast(FP8X4), scales=h_sc[b][:], in_=h_bf[b][:].rearrange("p n t -> p (n t)")
             )
-            cuts = 2 if b == 0 else 1
-            for a in range(cuts):
-                n = U // cuts
-                bank = psum.tile([P, n // D, D], F32, name="y_ps%d%d" % (b, a), tag="bank%d" % (BLOCKS + b if a == 0 else 0))
+            passes = [(0, 128, BLOCKS), (128, 256, 0), (256, U, 1)] if b == 0 else [(0, U, BLOCKS + b)]
+            for lo, hi, at in passes:
+                bank = psum.tile([P, (hi - lo) // D, D], F32, name="y_ps%d_%d" % (b, lo), tag="bank%d" % at)
                 nc.tensor.matmul_mx(
                     out=bank[:].rearrange("p v d -> p (v d)"),
                     lhsT=h_q[b][:].bitcast(FP8X4),
                     lhsT_scale=h_sc[b][:],
-                    rhs=e_q[:, a * n : (a + 1) * n].bitcast(FP8X4),
-                    rhs_scale=e_sc[:, a * n : (a + 1) * n],
+                    rhs=e_q[:, lo:hi].bitcast(FP8X4),
+                    rhs_scale=e_sc[:, lo:hi],
                     start=True,
                     stop=True,
                 )
-                y_ps[b, a] = bank
+                y_ps[b, lo // D] = bank
 
         def scores_of(i):
             b, vs = parts[i]
-            if b == 0:
-                a = vs.start // (V // 2)
-                return y_ps[b, a][:, vs.start - a * V // 2 : vs.stop - a * V // 2, :]
-            return y_ps[b, 0][:, vs, :]
+            return y_ps[b, vs.start][:] if b == 0 else y_ps[b, 0][:, vs, :]
 
         last = BLOCKS - 1
         cuts = [[0, 32, 64, V], [0, 64, V], [0, 64, V], [0, 32, 64, 96, V]]
@@ -163,8 +165,8 @@ def tile_picked_ytop1_bpr_p_kernel(
         sg = [keep.tile([P, D, V], F32, name="sg%d" % b) for b in range(BLOCKS)]
         top = []
         for i, (b, vs) in enumerate(parts):
-            if i == 1:
-                top.append(late.tile([P, vs.stop - vs.start], F32, name="top%d" % i, offset=4 * P * last, align_bytes=64))
+            if i in (0, 2):
+                top.append(late.tile([P, vs.stop - vs.start], F32, name="top%d" % i, offset=E_AT + 4 * P * (2 + i // 2), align_bytes=64))
             else:
                 top.append(keep.tile([P, vs.stop - vs.start], F32, name="top%d" % i))
         shift = [keep.tile([P, vs.stop - vs.start], F32, name="shift%d" % i) for i, (b, vs) in enumerate(parts)]
@@ -199,14 +201,14 @@ def tile_picked_ytop1_bpr_p_kernel(
             hidden(b)
         scores(0)
         scores(1)
-        scores(2)
         largest(0)
         choose_shift(0)
+        scores(2)
         for i in range(1, len(parts)):
             largest(i)
             shifted(i - 1)
             choose_shift(i)
-            if i == 1:
+            if i == 2:
                 scores(last)
         shifted(len(parts) - 1)
 
@@ -220,7 +222,9 @@ def tile_picked_ytop1_bpr_p_kernel(
         add_turned(sum_sg[1][:, 0, :], sg[last], range(D))
 
         both = [keep.tile([P, 2, P], F32, name="both%d" % b) for b in range(BLOCKS)]
-        back = []
+        runs = [range(0, 2), range(2, 3), range(3, 4)]
+        back = [psum.tile([P, len(run), 2, V], F32, name="back%d" % r, tag="bank%d" % (BLOCKS + r)) for r, run in enumerate(runs)]
+        back_of = {b: back[r][:, b - run.start] for r, run in enumerate(runs) for b in run}
 
         def scale_total(b):
             nc.vector.tensor_scalar(
@@ -229,18 +233,18 @@ def tile_picked_ytop1_bpr_p_kernel(
 
         def add_total(b):
             nc.vector.tensor_tensor(both[b][:, 1], sum_sg[b // last][:, b % last, :], both[b][:, 0], ALU.add)
-            back.append(psum.tile([P, 2, V], F32, name="back%d" % b, tag="bank%d" % (BLOCKS + b)))
             for i in range(2):
-                nc.tensor.transpose(back[b][:, i, :], both[b][:, i, :], ident[:])
+                nc.tensor.transpose(back_of[b][:, i, :], both[b][:, i, :], ident[:])
 
         scale_total(0)
         for b in range(1, BLOCKS):
             scale_total(b)
             add_total(b - 1)
         add_total(last)
-        for b in range(BLOCKS):
-            logs = keep.tile([P, 2, V], F32, name="logs%d" % b)
-            nc.scalar.activation(out=logs[:], in_=back[b][:], func=ACT.Ln)
-            res = keep.tile([P, V], F32, name="res%d" % b)
-            nc.vector.scalar_tensor_tensor(res[:], logs[:, 0], -math.log(EPS), logs[:, 1], ALU.add, ALU.subtract)
-            nc.sync.dma_start(out=out[b * P : (b + 1) * P, :], in_=res[:])
+        out_rows = out.rearrange("(b p) v -> p b v", p=P)
+        for r, run in enumerate(runs):
+            logs = keep.tile([P, len(run), 2, V], F32, name="logs%d" % r)
+            nc.scalar.activation(out=logs[:], in_=back[r][:], func=ACT.Ln)
+            res = keep.tile([P, len(run), V], F32, name="res%d" % r)
+            nc.vector.scalar_tensor_tensor(res[:], logs[:, :, 0], -math.log(EPS), logs[:, :, 1], ALU.add, ALU.subtract)
+            nc.sync.dma_start(out=out_rows[:, run.start : run.stop, :], in_=res[:])

@@ -100,12 +100,6 @@ def tile_picked_ytop1_bpr_p_kernel(
         w_sc = keep.tile([P, H], U8, name="w_sc", align_bytes=64)
         place_scale_rows(nc.sync, e_sc, e_sc_list)
         nc.vector.quantize_mx(out=w_q[:].bitcast(FP8X4), scales=w_sc[:], in_=w_bf[:, : PACK * H])
-        warm = psum.tile([P, H], F32, name="warm", tag="bank7")
-        for i in range(2):
-            nc.tensor.matmul_mx(
-                out=warm[:], lhsT=w_q[:, :P].bitcast(FP8X4), lhsT_scale=w_sc[:, :P], rhs=w_q[:].bitcast(FP8X4), rhs_scale=w_sc[:], start=True, stop=True
-            )
-
         x_q = []
 
         def gather_x(a):
@@ -158,7 +152,7 @@ def tile_picked_ytop1_bpr_p_kernel(
             return y_ps[b, vs.start][:] if b == 0 else y_ps[b, 0][:, vs, :]
 
         last = BLOCKS - 1
-        cuts = [[0, 32, 64, V], [0, 64, V], [0, 64, V], [0, 32, 64, 96, V]]
+        cuts = [[0, 32, 64, V], [0, 64, V], [0, 64, V], [0, 64, V]]
         parts = [(b, slice(c[i], c[i + 1])) for b, c in enumerate(cuts) for i in range(len(c) - 1)]
         u = [keep.tile([P, D, vs.stop - vs.start], F32, name="u%d" % i) for i, (b, vs) in enumerate(parts)]
         ex = [keep.tile([P, D, V], F32, name="ex%d" % b) for b in range(BLOCKS)]
@@ -178,16 +172,17 @@ def tile_picked_ytop1_bpr_p_kernel(
             b, vs = parts[i]
             nc.vector.scalar_tensor_tensor(shift[i][:], top[i][:], REACH, pos_sb[:, b, vs], ALU.add, ALU.min)
 
-        def shifted(i):
+        def shifted(i, lo, hi):
             b, vs = parts[i]
             nc.vector.tensor_tensor(
-                u[i][:],
-                scores_of(i).rearrange("p v d -> p d v"),
-                shift[i][:].unsqueeze(1).to_broadcast([P, D, vs.stop - vs.start]),
+                u[i][:, :, lo:hi],
+                scores_of(i)[:, lo:hi, :].rearrange("p v d -> p d v"),
+                shift[i][:, lo:hi].unsqueeze(1).to_broadcast([P, D, hi - lo]),
                 ALU.subtract,
             )
-            nc.scalar.activation(out=ex[b][:, :, vs], in_=u[i][:], func=ACT.Sigmoid, bias=-KNEE)
-            nc.scalar.activation(out=sg[b][:, :, vs], in_=u[i][:], func=ACT.Sigmoid)
+            cols = slice(vs.start + lo, vs.start + hi)
+            nc.scalar.activation(out=ex[b][:, :, cols], in_=u[i][:, :, lo:hi], func=ACT.Sigmoid, bias=-KNEE)
+            nc.scalar.activation(out=sg[b][:, :, cols], in_=u[i][:, :, lo:hi], func=ACT.Sigmoid)
 
         def add_turned(dst, src, ds):
             for d in ds:
@@ -204,13 +199,19 @@ def tile_picked_ytop1_bpr_p_kernel(
         largest(0)
         choose_shift(0)
         scores(2)
-        for i in range(1, len(parts)):
+        end = len(parts) - 1
+        for i in range(1, end):
             largest(i)
-            shifted(i - 1)
+            shifted(i - 1, 0, parts[i - 1][1].stop - parts[i - 1][1].start)
             choose_shift(i)
             if i == 2:
                 scores(last)
-        shifted(len(parts) - 1)
+        largest(end)
+        shifted(end - 1, 0, 32)
+        choose_shift(end)
+        shifted(end - 1, 32, 64)
+        shifted(end, 0, 32)
+        shifted(end, 32, 64)
 
         pieces = [range(0, last), range(last, BLOCKS)]
         sum_ex = [psum.tile([P, len(pieces[a]), P], F32, name="sum_ex%d" % a, tag="bank%d" % (2 * a)) for a in range(2)]

@@ -24,9 +24,10 @@ REACH = 24.0
 KNEE = 32.0
 EPS = 1e-3
 W_CUTS = [(0, 128), (128, 320), (320, 512)]
-E_AT = 4 * BLOCKS * V
-XS_AT = E_AT - T // 2
+E_AT = 0
+XS_AT = E_AT
 W_AT = E_AT + 4 * W
+POS_AT = W_AT + 2 * PACK * H
 
 
 ROWS_AT = P - 16
@@ -84,10 +85,8 @@ def tile_picked_ytop1_bpr_p_kernel(
         nc.vector.tensor_copy(x_sc_list[:], xs_tab[:].indirect(offs_t[:]))
         place_scale_rows(nc.sync, x_sc, x_sc_list)
         nc.sync.dma_start(out=e_tab[:].bitcast(I32), in_=e_words[0].rearrange("p n t -> p (n t)").bitcast(I32))
-        pos_sb = late.tile([P, BLOCKS, V], F32, name="pos_sb", offset=0, align_bytes=64)
-        nc.sync.dma_start(out=pos_sb[:], in_=pos.rearrange("(b p) v -> p b v", p=P))
 
-        w_bf = late.tile([P, PACK * H], BF16, name="w_bf", offset=W_AT, align_bytes=64)
+        w_bf = late.tile([P, PACK * H + 32], BF16, name="w_bf", offset=W_AT, align_bytes=64)
         w_dst = w_bf[:, : PACK * H].rearrange("p (t m j) -> p m j t", t=PACK, j=PACK)
         for i, (a, b) in enumerate(W_CUTS):
             nc.scalar.activation(
@@ -100,6 +99,8 @@ def tile_picked_ytop1_bpr_p_kernel(
         w_sc = keep.tile([P, H], U8, name="w_sc", align_bytes=64)
         place_scale_rows(nc.sync, e_sc, e_sc_list)
         nc.vector.quantize_mx(out=w_q[:].bitcast(FP8X4), scales=w_sc[:], in_=w_bf[:, : PACK * H])
+        pos_sb = late.tile([P, BLOCKS, V], F32, name="pos_sb", offset=POS_AT, align_bytes=64)
+        nc.sync.dma_start(out=pos_sb[:], in_=pos.rearrange("(b p) v -> p b v", p=P))
         x_q = []
 
         def gather_x(a):

@@ -87,10 +87,10 @@ def tile_picked_ytop1_bpr_p_kernel(
         nc.sync.dma_start(out=e_tab[:].bitcast(I32), in_=e_words[0].rearrange("p n t -> p (n t)").bitcast(I32))
 
         w_bf = late.tile([P, PACK * H + 32], BF16, name="w_bf", offset=W_AT, align_bytes=64)
-        w_dst = w_bf[:, : PACK * H].rearrange("p (t m j) -> p m j t", t=PACK, j=PACK)
+        w_dst = w_bf[:, : PACK * H].rearrange("p (t m j) -> p m t j", t=PACK, j=PACK)
         for i, (a, b) in enumerate(W_CUTS):
             nc.scalar.activation(
-                out=w_dst[:, a // PACK : b // PACK], in_=w_raw[i][:].rearrange("p j (m t) -> p m j t", t=PACK), func=ACT.Copy
+                out=w_dst[:, a // PACK : b // PACK], in_=w_raw[i][:].rearrange("p j (m t) -> p m t j", t=PACK), func=ACT.Copy
             )
 
         e_sc_list = keep.tile([P, U], U8, name="e_sc_list", align_bytes=64)
@@ -224,7 +224,7 @@ def tile_picked_ytop1_bpr_p_kernel(
         add_turned(sum_sg[1][:, 0, :], sg[last], range(D))
 
         both = [keep.tile([P, 2, P], F32, name="both%d" % b) for b in range(BLOCKS)]
-        runs = [range(0, 2), range(2, 3), range(3, 4)]
+        runs = [range(b, b + 1) for b in range(BLOCKS)]
         back = [psum.tile([P, len(run), 2, V], F32, name="back%d" % r, tag="bank%d" % (BLOCKS + r)) for r, run in enumerate(runs)]
         back_of = {b: back[r][:, b - run.start] for r, run in enumerate(runs) for b in run}
 

@@ -24,10 +24,12 @@ REACH = 24.0
 KNEE = 32.0
 EPS = 1e-3
 W_CUTS = [(0, 128), (128, 320), (320, 512)]
+W_SHARE = 448
 E_AT = 0
 XS_AT = E_AT
 W_AT = E_AT + 4 * W
 POS_AT = W_AT + 2 * PACK * H
+BOTH_AT = POS_AT + 4 * BLOCKS * V
 
 
 ROWS_AT = P - 16
@@ -88,13 +90,14 @@ def tile_picked_ytop1_bpr_p_kernel(
 
         w_bf = late.tile([P, PACK * H + 32], BF16, name="w_bf", offset=W_AT, align_bytes=64)
         w_dst = w_bf[:, : PACK * H].rearrange("p (t m j) -> p m t j", t=PACK, j=PACK)
+        w_src = [raw[:].rearrange("p j (m t) -> p m t j", t=PACK) for raw in w_raw]
         for i, (a, b) in enumerate(W_CUTS):
-            nc.scalar.activation(
-                out=w_dst[:, a // PACK : b // PACK], in_=w_raw[i][:].rearrange("p j (m t) -> p m t j", t=PACK), func=ACT.Copy
-            )
+            end = min(b, W_SHARE)
+            nc.scalar.activation(out=w_dst[:, a // PACK : end // PACK], in_=w_src[i][:, : (end - a) // PACK], func=ACT.Copy)
 
         e_sc_list = keep.tile([P, U], U8, name="e_sc_list", align_bytes=64)
         nc.vector.tensor_copy(e_sc_list[:], es_tab[:].indirect(neg_t[:]))
+        nc.vector.tensor_copy(w_dst[:, W_SHARE // PACK :], w_src[2][:, (W_SHARE - W_CUTS[2][0]) // PACK :])
         w_q = keep.tile([P, H], U32, name="w_q", align_bytes=64)
         w_sc = keep.tile([P, H], U8, name="w_sc", align_bytes=64)
         place_scale_rows(nc.sync, e_sc, e_sc_list)
@@ -108,9 +111,14 @@ def tile_picked_ytop1_bpr_p_kernel(
             nc.vector.tensor_copy(words[:], x_tab[:].indirect(offs_half[a]))
             x_q.append(words)
 
-        h_q = [late.tile([P, P], U32, name="h_q%d" % b, offset=E_AT + 4 * P * b, align_bytes=64) for b in range(BLOCKS)]
-        h_sc = [keep.tile([P, P], U8, name="h_sc%d" % b, align_bytes=64) for b in range(BLOCKS)]
-        h_bf = {}
+        h_q = [late.tile([P, P], U32, name="h_q%d" % b, offset=E_AT + 4 * P * b, align_bytes=64)[:] for b in range(2)]
+        h_sc = [keep.tile([P, P], U8, name="h_sc%d" % b, align_bytes=64)[:] for b in range(2)]
+        h_q_late = late.tile([P, 2 * P], U32, name="h_q_late", offset=E_AT + 8 * P, align_bytes=64)
+        h_sc_late = keep.tile([P, 2 * P], U8, name="h_sc_late", align_bytes=64)
+        h_bf_late = keep.tile([P, 2 * P, PACK], BF16, name="h_bf_late", align_bytes=64)
+        h_q.extend([h_q_late[:, :P], h_q_late[:, P:]])
+        h_sc.extend([h_sc_late[:, :P], h_sc_late[:, P:]])
+        h_bf = {2: h_bf_late[:, :P, :], 3: h_bf_late[:, P:, :]}
         y_ps = {}
 
         def hidden(b):
@@ -127,20 +135,24 @@ def tile_picked_ytop1_bpr_p_kernel(
                     start=True,
                     stop=True,
                 )
-            h_bf[b] = keep.tile([P, P, PACK], BF16, name="h_bf%d" % b, align_bytes=64)
-            nc.scalar.copy(out=h_bf[b][:], in_=h_ps[:].rearrange("p t n -> p n t"))
+            if b < 2:
+                h_bf[b] = keep.tile([P, P, PACK], BF16, name="h_bf%d" % b, align_bytes=64)[:]
+            nc.scalar.copy(out=h_bf[b], in_=h_ps[:].rearrange("p t n -> p n t"))
 
         def scores(b):
-            nc.vector.quantize_mx(
-                out=h_q[b][:].bitcast(FP8X4), scales=h_sc[b][:], in_=h_bf[b][:].rearrange("p n t -> p (n t)")
-            )
+            if b < 2:
+                nc.vector.quantize_mx(out=h_q[b].bitcast(FP8X4), scales=h_sc[b], in_=h_bf[b].rearrange("p n t -> p (n t)"))
+            if b == 2:
+                nc.vector.quantize_mx(
+                    out=h_q_late[:].bitcast(FP8X4), scales=h_sc_late[:], in_=h_bf_late[:].rearrange("p n t -> p (n t)")
+                )
             passes = [(0, 128, BLOCKS), (128, 256, 0), (256, U, 1)] if b == 0 else [(0, U, BLOCKS + b)]
             for lo, hi, at in passes:
                 bank = psum.tile([P, (hi - lo) // D, D], F32, name="y_ps%d_%d" % (b, lo), tag="bank%d" % at)
                 nc.tensor.matmul_mx(
                     out=bank[:].rearrange("p v d -> p (v d)"),
-                    lhsT=h_q[b][:].bitcast(FP8X4),
-                    lhsT_scale=h_sc[b][:],
+                    lhsT=h_q[b].bitcast(FP8X4),
+                    lhsT_scale=h_sc[b],
                     rhs=e_q[:, lo:hi].bitcast(FP8X4),
                     rhs_scale=e_sc[:, lo:hi],
                     start=True,
@@ -156,12 +168,14 @@ def tile_picked_ytop1_bpr_p_kernel(
         cuts = [[0, 32, 64, V], [0, 64, V], [0, 64, V], [0, 64, V]]
         parts = [(b, slice(c[i], c[i + 1])) for b, c in enumerate(cuts) for i in range(len(c) - 1)]
         u = [keep.tile([P, D, vs.stop - vs.start], F32, name="u%d" % i) for i, (b, vs) in enumerate(parts)]
-        ex = [keep.tile([P, D, V], F32, name="ex%d" % b) for b in range(BLOCKS)]
+        ex = [keep.tile([P, D, V], F32, name="ex%d" % b) for b in range(2)]
+        ex.append(late.tile([P, D, V], F32, name="ex2", offset=BOTH_AT, align_bytes=64))
+        ex.append(keep.tile([P, D, V], F32, name="ex3"))
         sg = [keep.tile([P, D, V], F32, name="sg%d" % b) for b in range(BLOCKS)]
         top = []
         for i, (b, vs) in enumerate(parts):
-            if i in (0, 2):
-                top.append(late.tile([P, vs.stop - vs.start], F32, name="top%d" % i, offset=E_AT + 4 * P * (2 + i // 2), align_bytes=64))
+            if i == 1:
+                top.append(late.tile([P, vs.stop - vs.start], F32, name="top%d" % i, offset=E_AT + 8 * P, align_bytes=64))
             else:
                 top.append(keep.tile([P, vs.stop - vs.start], F32, name="top%d" % i))
         shift = [keep.tile([P, vs.stop - vs.start], F32, name="shift%d" % i) for i, (b, vs) in enumerate(parts)]
@@ -199,13 +213,13 @@ def tile_picked_ytop1_bpr_p_kernel(
         scores(1)
         largest(0)
         choose_shift(0)
-        scores(2)
         end = len(parts) - 1
         for i in range(1, end):
             largest(i)
             shifted(i - 1, 0, parts[i - 1][1].stop - parts[i - 1][1].start)
             choose_shift(i)
-            if i == 2:
+            if i == 1:
+                scores(2)
                 scores(last)
         largest(end)
         shifted(end - 1, 0, 32)
@@ -214,27 +228,29 @@ def tile_picked_ytop1_bpr_p_kernel(
         shifted(end, 0, 32)
         shifted(end, 32, 64)
 
-        pieces = [range(0, last), range(last, BLOCKS)]
-        sum_ex = [psum.tile([P, len(pieces[a]), P], F32, name="sum_ex%d" % a, tag="bank%d" % (2 * a)) for a in range(2)]
-        sum_sg = [psum.tile([P, len(pieces[a]), P], F32, name="sum_sg%d" % a, tag="bank%d" % (2 * a + 1)) for a in range(2)]
-        for b in range(last):
-            add_turned(sum_ex[0][:, b, :], ex[b], range(D))
-            add_turned(sum_sg[0][:, b, :], sg[b], range(D))
-        add_turned(sum_ex[1][:, 0, :], ex[last], range(D))
-        add_turned(sum_sg[1][:, 0, :], sg[last], range(D))
+        early_ex = psum.tile([P, 2, P], F32, name="early_ex", tag="bank0")
+        early_sg = psum.tile([P, 2, P], F32, name="early_sg", tag="bank1")
+        third = psum.tile([P, 2, P], F32, name="third", tag="bank2")
+        last_ex = psum.tile([P, P], F32, name="last_ex", tag="bank3")
+        last_sg = psum.tile([P, P], F32, name="last_sg", tag="bank4")
+        sum_ex = [early_ex[:, 0, :], early_ex[:, 1, :], third[:, 0, :], last_ex[:]]
+        sum_sg = [early_sg[:, 0, :], early_sg[:, 1, :], third[:, 1, :], last_sg[:]]
+        for b in range(BLOCKS):
+            add_turned(sum_ex[b], ex[b], range(D))
+            add_turned(sum_sg[b], sg[b], range(D))
 
-        both = [keep.tile([P, 2, P], F32, name="both%d" % b) for b in range(BLOCKS)]
+        both = [late.tile([P, 2, P], F32, name="both%d" % b, offset=BOTH_AT + 8 * P * b, align_bytes=64) for b in range(BLOCKS)]
         runs = [range(b, b + 1) for b in range(BLOCKS)]
-        back = [psum.tile([P, len(run), 2, V], F32, name="back%d" % r, tag="bank%d" % (BLOCKS + r)) for r, run in enumerate(runs)]
-        back_of = {b: back[r][:, b - run.start] for r, run in enumerate(runs) for b in run}
+        back = [psum.tile([P, 1, 2, V], F32, name="back%d" % b, tag="bank%d" % (BLOCKS + b if b else 0)) for b in range(BLOCKS)]
+        back_of = {b: back[b][:, 0] for b in range(BLOCKS)}
 
         def scale_total(b):
             nc.vector.tensor_scalar(
-                both[b][:, 0], sum_ex[b // last][:, b % last, :], half_one[:], 2.0 * EPS * math.exp(KNEE), ALU.mult, ALU.mult
+                both[b][:, 0], sum_ex[b], half_one[:], 2.0 * EPS * math.exp(KNEE), ALU.mult, ALU.mult
             )
 
         def add_total(b):
-            nc.vector.tensor_tensor(both[b][:, 1], sum_sg[b // last][:, b % last, :], both[b][:, 0], ALU.add)
+            nc.vector.tensor_tensor(both[b][:, 1], sum_sg[b], both[b][:, 0], ALU.add)
             for i in range(2):
                 nc.tensor.transpose(back_of[b][:, i, :], both[b][:, i, :], ident[:])
 

@@ -23,7 +23,7 @@ BLOCKS = S // P
 REACH = 24.0
 KNEE = 32.0
 EPS = 1e-3
-W_CUTS = [(0, 128), (128, 320), (320, 512)]
+W_CUTS = [(0, 128), (128, 384), (384, 512)]
 W_SHARE = 448
 E_AT = 0
 XS_AT = E_AT

@@ -23,7 +23,7 @@ BLOCKS = S // P
 REACH = 24.0
 KNEE = 32.0
 EPS = 1e-3
-W_CUTS = [(0, 128), (128, 384), (384, 512)]
+W_CUTS = [(0, 192), (192, 384), (384, 512)]
 W_SHARE = 448
 E_AT = 0
 XS_AT = E_AT
@@ -32,14 +32,15 @@ POS_AT = W_AT + 2 * PACK * H
 BOTH_AT = POS_AT + 4 * BLOCKS * V
 
 
-ROWS_AT = P - 16
+ROWS_AT = 32
+ROW_STEP = 4
 
 
 def place_scale_rows(engine, plane, picked):
     dst = plane[:].bitcast(I32)
     src = picked[:].bitcast(I32)
     for q in range(4):
-        engine.dma_start(out=dst[32 * q : 32 * q + 4, :], in_=src[ROWS_AT + 4 * q : ROWS_AT + 4 * q + 4, :])
+        engine.dma_start(out=dst[32 * q : 32 * q + 4, :], in_=src[ROWS_AT + 4 * ROW_STEP * q : ROWS_AT + 4 * ROW_STEP * (q + 1) : ROW_STEP, :])
 
 
 def tile_picked_ytop1_bpr_p_kernel(
@@ -63,9 +64,9 @@ def tile_picked_ytop1_bpr_p_kernel(
 
         x_sc = keep.tile([P, S], U8, name="x_sc", align_bytes=64)
         e_sc = keep.tile([P, U], U8, name="e_sc", align_bytes=64)
+        nc.gpsimd.memset(xs_tab[:].bitcast(I32), 0)
+        nc.vector.memset(es_tab[:].bitcast(I32), 0)
         nc.vector.memset(zero[:], 0.0)
-        for table in (xs_tab, es_tab):
-            nc.vector.memset(table[:].bitcast(I32)[:ROWS_AT, :], 0)
         for plane in (x_sc, e_sc):
             nc.vector.memset(plane[:].bitcast(I32), 0)
         half_one = keep.tile([P, 1], F32, name="half_one")
@@ -73,9 +74,9 @@ def tile_picked_ytop1_bpr_p_kernel(
         w_rows = w1.rearrange("(p j) c -> p j c", j=PACK)
         nc.sync.dma_start(out=w_raw[0][:], in_=w_rows[:, :, : W_CUTS[0][1]])
         nc.sync.dma_start(offs_t[:], offs)
-        nc.sync.dma_start(out=xs_tab[:].bitcast(I32)[ROWS_AT:, :], in_=x_scales[0].bitcast(I32))
         nc.sync.dma_start(neg_t[:], neg)
-        nc.sync.dma_start(out=es_tab[:].bitcast(I32)[ROWS_AT:, :], in_=e_scales[0].bitcast(I32))
+        nc.sync.dma_start(out=xs_tab[:].bitcast(I32)[ROWS_AT : ROWS_AT + 16 * ROW_STEP : ROW_STEP, :], in_=x_scales[0].bitcast(I32))
+        nc.sync.dma_start(out=es_tab[:].bitcast(I32)[ROWS_AT : ROWS_AT + 16 * ROW_STEP : ROW_STEP, :], in_=e_scales[0].bitcast(I32))
         for i in (1, 2):
             nc.sync.dma_start(out=w_raw[i][:], in_=w_rows[:, :, W_CUTS[i][0] : W_CUTS[i][1]])
         nc.sync.dma_start(out=x_tab[:].bitcast(I32), in_=x_words[0].rearrange("p n t -> p (n t)").bitcast(I32))

@@ -36,6 +36,13 @@ ROWS_AT = 32
 ROW_STEP = 4
 
 
+QUARTER = 32
+
+
+def dealt(tile):
+    return tile[:].rearrange("p (q d v) -> p q v d", d=D, v=QUARTER)
+
+
 def place_scale_rows(engine, plane, picked):
     dst = plane[:].bitcast(I32)
     src = picked[:].bitcast(I32)
@@ -97,7 +104,7 @@ def tile_picked_ytop1_bpr_p_kernel(
             nc.scalar.activation(out=w_dst[:, a // PACK : end // PACK], in_=w_src[i][:, : (end - a) // PACK], func=ACT.Copy)
 
         e_sc_list = keep.tile([P, U], U8, name="e_sc_list", align_bytes=64)
-        nc.vector.tensor_copy(e_sc_list[:], es_tab[:].indirect(neg_t[:]))
+        nc.vector.tensor_copy(dealt(e_sc_list), es_tab[:].indirect(neg_t[:]))
         nc.vector.tensor_copy(w_dst[:, W_SHARE // PACK :], w_src[2][:, (W_SHARE - W_CUTS[2][0]) // PACK :])
         w_q = keep.tile([P, H], U32, name="w_q", align_bytes=64)
         w_sc = keep.tile([P, H], U8, name="w_sc", align_bytes=64)
@@ -149,9 +156,9 @@ def tile_picked_ytop1_bpr_p_kernel(
                 )
             passes = [(0, 128, BLOCKS), (128, 256, 0), (256, U, 1)] if b == 0 else [(0, U, BLOCKS + b)]
             for lo, hi, at in passes:
-                bank = psum.tile([P, (hi - lo) // D, D], F32, name="y_ps%d_%d" % (b, lo), tag="bank%d" % at)
+                bank = psum.tile([P, (hi - lo) // (D * QUARTER), D, QUARTER], F32, name="y_ps%d_%d" % (b, lo), tag="bank%d" % at)
                 nc.tensor.matmul_mx(
-                    out=bank[:].rearrange("p v d -> p (v d)"),
+                    out=bank[:].rearrange("p q d v -> p (q d v)"),
                     lhsT=h_q[b].bitcast(FP8X4),
                     lhsT_scale=h_sc[b],
                     rhs=e_q[:, lo:hi].bitcast(FP8X4),
@@ -163,7 +170,7 @@ def tile_picked_ytop1_bpr_p_kernel(
 
         def scores_of(i):
             b, vs = parts[i]
-            return y_ps[b, vs.start][:] if b == 0 else y_ps[b, 0][:, vs, :]
+            return y_ps[b, vs.start][:] if b == 0 else y_ps[b, 0][:, vs.start // QUARTER : vs.stop // QUARTER]
 
         last = BLOCKS - 1
         cuts = [[0, 32, 64, V], [0, 64, V], [0, 64, V], [0, 64, V]]
@@ -182,7 +189,7 @@ def tile_picked_ytop1_bpr_p_kernel(
         shift = [keep.tile([P, vs.stop - vs.start], F32, name="shift%d" % i) for i, (b, vs) in enumerate(parts)]
 
         def largest(i):
-            nc.vector.tensor_reduce(out=top[i][:], in_=scores_of(i), axis=mybir.AxisListType.X, op=ALU.max)
+            nc.vector.tensor_reduce(out=top[i][:].rearrange("p (q v) -> p q v", v=QUARTER), in_=scores_of(i).rearrange("p q d v -> p q v d"), axis=mybir.AxisListType.X, op=ALU.max)
 
         def choose_shift(i):
             b, vs = parts[i]
@@ -191,9 +198,9 @@ def tile_picked_ytop1_bpr_p_kernel(
         def shifted(i, lo, hi):
             b, vs = parts[i]
             nc.vector.tensor_tensor(
-                u[i][:, :, lo:hi],
-                scores_of(i)[:, lo:hi, :].rearrange("p v d -> p d v"),
-                shift[i][:, lo:hi].unsqueeze(1).to_broadcast([P, D, hi - lo]),
+                u[i][:, :, lo:hi].rearrange("p d (q v) -> p q d v", v=QUARTER),
+                scores_of(i)[:, lo // QUARTER : hi // QUARTER],
+                shift[i][:, lo:hi].rearrange("p (q v) -> p q v", v=QUARTER).unsqueeze(2).to_broadcast([P, (hi - lo) // QUARTER, D, QUARTER]),
                 ALU.subtract,
             )
             cols = slice(vs.start + lo, vs.start + hi)
@@ -207,7 +214,7 @@ def tile_picked_ytop1_bpr_p_kernel(
         gather_x(0)
         gather_x(1)
         e_q = late.tile([P, U], U32, name="e_q", offset=W_AT + 4 * S, align_bytes=64)
-        nc.vector.tensor_copy(e_q[:], e_tab[:].indirect(neg_t[:]))
+        nc.vector.tensor_copy(dealt(e_q), e_tab[:].indirect(neg_t[:]))
         for b in range(BLOCKS):
             hidden(b)
         scores(0)

import math
from contextlib import ExitStack

import concourse.mybir as mybir
from concourse.masks import make_identity

K, T, S, H, D, V, W, U = 512, 2048, 512, 512, 4, 128, 1024, 512
FLOPS = 2 * K * H * S + 2 * H * S * U

F32 = mybir.dt.float32
BF16 = mybir.dt.bfloat16
I32 = mybir.dt.int32
U32 = mybir.dt.uint32
U16 = mybir.dt.uint16
U8 = mybir.dt.uint8
FP8X4 = mybir.dt.float8_e4m3fn_x4
ALU = mybir.AluOpType
ACT = mybir.ActivationFunctionType

P = 128
PACK = 4
BLOCKS = S // P
REACH = 24.0
KNEE = 32.0
EPS = 1e-3
W_CUTS = [(0, 192), (192, 384), (384, 512)]
W_SHARE = 448
E_AT = 0
XS_AT = E_AT
W_AT = E_AT + 4 * W
POS_AT = W_AT + 2 * PACK * H
BOTH_AT = POS_AT + 4 * BLOCKS * V


ROWS_AT = 32
ROW_STEP = 4


QUARTER = 32


def dealt(tile):
    return tile[:].rearrange("p (q d v) -> p q v d", d=D, v=QUARTER)


def place_scale_rows(engine, plane, picked):
    dst = plane[:].bitcast(I32)
    src = picked[:].bitcast(I32)
    for q in range(4):
        engine.dma_start(out=dst[32 * q : 32 * q + 4, :], in_=src[ROWS_AT + 4 * ROW_STEP * q : ROWS_AT + 4 * ROW_STEP * (q + 1) : ROW_STEP, :])


def tile_picked_ytop1_bpr_p_kernel(
    tc, x_words, x_scales, w1, e_words, e_scales, pos, offs, neg, out
):
    nc = tc.nc
    with ExitStack() as ctx:
        keep = ctx.enter_context(tc.tile_pool(name="keep", bufs=1))
        psum = ctx.enter_context(tc.psum_pool(name="psum", bufs=1))
        late = ctx.enter_context(tc.tile_pool(name="late", bufs=1))

        offs_t = keep.tile([P, S // 16], U16, name="offs_t")
        neg_t = keep.tile([P, U // 16], U16, name="neg_t")
        w_raw = [keep.tile([P, PACK, b - a], F32, name="w_raw%d" % a) for a, b in W_CUTS]
        x_tab = keep.tile([P, T], U32, name="x_tab", align_bytes=64)
        e_tab = late.tile([P, W], U32, name="e_tab", offset=E_AT, align_bytes=64)
        xs_tab = late.tile([P, T], U8, name="xs_tab", offset=XS_AT, align_bytes=64)
        es_tab = keep.tile([P, W], U8, name="es_tab", align_bytes=64)
        ident = keep.tile([P, P], F32, name="ident")
        zero = keep.tile([P, 1], F32, name="zero")

        x_sc = keep.tile([P, S], U8, name="x_sc", align_bytes=64)
        e_sc = keep.tile([P, U], U8, name="e_sc", align_bytes=64)
        nc.gpsimd.memset(xs_tab[:].bitcast(I32), 0)
        nc.vector.memset(es_tab[:].bitcast(I32), 0)
        nc.vector.memset(zero[:], 0.0)
        for plane in (x_sc, e_sc):
            nc.vector.memset(plane[:].bitcast(I32), 0)
        half_one = keep.tile([P, 1], F32, name="half_one")
        nc.scalar.activation(out=half_one[:], in_=zero[:], func=ACT.Sigmoid)
        w_rows = w1.rearrange("(p j) c -> p j c", j=PACK)
        nc.sync.dma_start(out=w_raw[0][:], in_=w_rows[:, :, : W_CUTS[0][1]])
        nc.sync.dma_start(offs_t[:], offs)
        nc.sync.dma_start(neg_t[:], neg)
        nc.sync.dma_start(out=xs_tab[:].bitcast(I32)[ROWS_AT : ROWS_AT + 16 * ROW_STEP : ROW_STEP, :], in_=x_scales[0].bitcast(I32))
        nc.sync.dma_start(out=es_tab[:].bitcast(I32)[ROWS_AT : ROWS_AT + 16 * ROW_STEP : ROW_STEP, :], in_=e_scales[0].bitcast(I32))
        for i in (1, 2):
            nc.sync.dma_start(out=w_raw[i][:], in_=w_rows[:, :, W_CUTS[i][0] : W_CUTS[i][1]])
        nc.sync.dma_start(out=x_tab[:].bitcast(I32), in_=x_words[0].rearrange("p n t -> p (n t)").bitcast(I32))
        make_identity(nc, ident[:])

        half = S // 2
        offs_half = [offs_t[:, a * half // 16 : (a + 1) * half // 16] for a in range(2)]
        x_sc_list = keep.tile([P, S], U8, name="x_sc_list", align_bytes=64)
        nc.vector.tensor_copy(x_sc_list[:], xs_tab[:].indirect(offs_t[:]))
        place_scale_rows(nc.sync, x_sc, x_sc_list)
        nc.sync.dma_start(out=e_tab[:].bitcast(I32), in_=e_words[0].rearrange("p n t -> p (n t)").bitcast(I32))

        w_bf = late.tile([P, PACK * H + 32], BF16, name="w_bf", offset=W_AT, align_bytes=64)
        w_dst = w_bf[:, : PACK * H].rearrange("p (t m j) -> p m t j", t=PACK, j=PACK)
        w_src = [raw[:].rearrange("p j (m t) -> p m t j", t=PACK) for raw in w_raw]
        for i, (a, b) in enumerate(W_CUTS):
            end = min(b, W_SHARE)
            nc.scalar.activation(out=w_dst[:, a // PACK : end // PACK], in_=w_src[i][:, : (end - a) // PACK], func=ACT.Copy)

        e_sc_list = keep.tile([P, U], U8, name="e_sc_list", align_bytes=64)
        nc.vector.tensor_copy(dealt(e_sc_list), es_tab[:].indirect(neg_t[:]))
        nc.vector.tensor_copy(w_dst[:, W_SHARE // PACK :], w_src[2][:, (W_SHARE - W_CUTS[2][0]) // PACK :])
        w_q = keep.tile([P, H], U32, name="w_q", align_bytes=64)
        w_sc = keep.tile([P, H], U8, name="w_sc", align_bytes=64)
        place_scale_rows(nc.sync, e_sc, e_sc_list)
        nc.vector.quantize_mx(out=w_q[:].bitcast(FP8X4), scales=w_sc[:], in_=w_bf[:, : PACK * H])
        pos_sb = late.tile([P, BLOCKS, V], F32, name="pos_sb", offset=POS_AT, align_bytes=64)
        nc.sync.dma_start(out=pos_sb[:], in_=pos.rearrange("(b p) v -> p b v", p=P))
        x_q = []

        def gather_x(a):
            words = late.tile([P, half], U32, name="x_q%d" % a, offset=W_AT + 4 * half * a, align_bytes=64)
            nc.vector.tensor_copy(words[:], x_tab[:].indirect(offs_half[a]))
            x_q.append(words)

        h_q = [late.tile([P, P], U32, name="h_q%d" % b, offset=E_AT + 4 * P * b, align_bytes=64)[:] for b in range(2)]
        h_sc = [keep.tile([P, P], U8, name="h_sc%d" % b, align_bytes=64)[:] for b in range(2)]
        h_q_late = late.tile([P, 2 * P], U32, name="h_q_late", offset=E_AT + 8 * P, align_bytes=64)
        h_sc_late = keep.tile([P, 2 * P], U8, name="h_sc_late", align_bytes=64)
        h_bf_late = keep.tile([P, 2 * P, PACK], BF16, name="h_bf_late", align_bytes=64)
        h_q.extend([h_q_late[:, :P], h_q_late[:, P:]])
        h_sc.extend([h_sc_late[:, :P], h_sc_late[:, P:]])
        h_bf = {2: h_bf_late[:, :P, :], 3: h_bf_late[:, P:, :]}
        y_ps = {}

        def hidden(b):
            h_ps = psum.tile([P, PACK, P], F32, name="h_ps%d" % b, tag="bank%d" % b)
            cols = slice((b % 2) * P, (b % 2 + 1) * P)
            for t in range(PACK):
                wc = slice(t * P, (t + 1) * P)
                nc.tensor.matmul_mx(
                    out=h_ps[:, t, :],
                    lhsT=w_q[:, wc].bitcast(FP8X4),
                    lhsT_scale=w_sc[:, wc],
                    rhs=x_q[b // 2][:, cols].bitcast(FP8X4),
                    rhs_scale=x_sc[:, b * P : (b + 1) * P],
                    start=True,
                    stop=True,
                )
            if b < 2:
                h_bf[b] = keep.tile([P, P, PACK], BF16, name="h_bf%d" % b, align_bytes=64)[:]
            nc.scalar.copy(out=h_bf[b], in_=h_ps[:].rearrange("p t n -> p n t"))

        def scores(b):
            if b < 2:
                nc.vector.quantize_mx(out=h_q[b].bitcast(FP8X4), scales=h_sc[b], in_=h_bf[b].rearrange("p n t -> p (n t)"))
            if b == 2:
                nc.vector.quantize_mx(
                    out=h_q_late[:].bitcast(FP8X4), scales=h_sc_late[:], in_=h_bf_late[:].rearrange("p n t -> p (n t)")
                )
            passes = [(0, 128, BLOCKS), (128, 256, 0), (256, U, 1)] if b == 0 else [(0, U, BLOCKS + b)]
            for lo, hi, at in passes:
                bank = psum.tile([P, (hi - lo) // (D * QUARTER), D, QUARTER], F32, name="y_ps%d_%d" % (b, lo), tag="bank%d" % at)
                nc.tensor.matmul_mx(
                    out=bank[:].rearrange("p q d v -> p (q d v)"),
                    lhsT=h_q[b].bitcast(FP8X4),
                    lhsT_scale=h_sc[b],
                    rhs=e_q[:, lo:hi].bitcast(FP8X4),
                    rhs_scale=e_sc[:, lo:hi],
                    start=True,
                    stop=True,
                )
                y_ps[b, lo // D] = bank

        def scores_of(i):
            b, vs = parts[i]
            return y_ps[b, vs.start][:] if b == 0 else y_ps[b, 0][:, vs.start // QUARTER : vs.stop // QUARTER]

        last = BLOCKS - 1
        cuts = [[0, 32, 64, V], [0, 64, V], [0, 64, V], [0, 64, V]]
        parts = [(b, slice(c[i], c[i + 1])) for b, c in enumerate(cuts) for i in range(len(c) - 1)]
        u = [keep.tile([P, D, vs.stop - vs.start], F32, name="u%d" % i) for i, (b, vs) in enumerate(parts)]
        ex = [keep.tile([P, D, V], F32, name="ex%d" % b) for b in range(2)]
        ex.append(late.tile([P, D, V], F32, name="ex2", offset=BOTH_AT, align_bytes=64))
        ex.append(keep.tile([P, D, V], F32, name="ex3"))
        sg = [keep.tile([P, D, V], F32, name="sg%d" % b) for b in range(BLOCKS)]
        top = []
        for i, (b, vs) in enumerate(parts):
            if i == 1:
                top.append(late.tile([P, vs.stop - vs.start], F32, name="top%d" % i, offset=E_AT + 8 * P, align_bytes=64))
            else:
                top.append(keep.tile([P, vs.stop - vs.start], F32, name="top%d" % i))
        shift = [keep.tile([P, vs.stop - vs.start], F32, name="shift%d" % i) for i, (b, vs) in enumerate(parts)]

        def largest(i):
            nc.vector.tensor_reduce(out=top[i][:].rearrange("p (q v) -> p q v", v=QUARTER), in_=scores_of(i).rearrange("p q d v -> p q v d"), axis=mybir.AxisListType.X, op=ALU.max)

        def choose_shift(i):
            b, vs = parts[i]
            nc.vector.scalar_tensor_tensor(shift[i][:], top[i][:], REACH, pos_sb[:, b, vs], ALU.add, ALU.min)

        def shifted(i, lo, hi):
            b, vs = parts[i]
            nc.vector.tensor_tensor(
                u[i][:, :, lo:hi].rearrange("p d (q v) -> p q d v", v=QUARTER),
                scores_of(i)[:, lo // QUARTER : hi // QUARTER],
                shift[i][:, lo:hi].rearrange("p (q v) -> p q v", v=QUARTER).unsqueeze(2).to_broadcast([P, (hi - lo) // QUARTER, D, QUARTER]),
                ALU.subtract,
            )
            cols = slice(vs.start + lo, vs.start + hi)
            nc.scalar.activation(out=ex[b][:, :, cols], in_=u[i][:, :, lo:hi], func=ACT.Sigmoid, bias=-KNEE)
            nc.scalar.activation(out=sg[b][:, :, cols], in_=u[i][:, :, lo:hi], func=ACT.Sigmoid)

        def add_turned(dst, src, ds):
            for d in ds:
                nc.tensor.matmul(dst, src[:, d, :], ident[:], start=(d == 0), stop=(d == D - 1), is_transpose=True)

        gather_x(0)
        gather_x(1)
        e_q = late.tile([P, U], U32, name="e_q", offset=W_AT + 4 * S, align_bytes=64)
        nc.vector.tensor_copy(dealt(e_q), e_tab[:].indirect(neg_t[:]))
        for b in range(BLOCKS):
            hidden(b)
        scores(0)
        scores(1)
        largest(0)
        choose_shift(0)
        end = len(parts) - 1
        for i in range(1, end):
            largest(i)
            shifted(i - 1, 0, parts[i - 1][1].stop - parts[i - 1][1].start)
            choose_shift(i)
            if i == 1:
                scores(2)
                scores(last)
        largest(end)
        shifted(end - 1, 0, 32)
        choose_shift(end)
        shifted(end - 1, 32, 64)
        shifted(end, 0, 32)
        shifted(end, 32, 64)

        early_ex = psum.tile([P, 2, P], F32, name="early_ex", tag="bank0")
        early_sg = psum.tile([P, 2, P], F32, name="early_sg", tag="bank1")
        third = psum.tile([P, 2, P], F32, name="third", tag="bank2")
        last_ex = psum.tile([P, P], F32, name="last_ex", tag="bank3")
        last_sg = psum.tile([P, P], F32, name="last_sg", tag="bank4")
        sum_ex = [early_ex[:, 0, :], early_ex[:, 1, :], third[:, 0, :], last_ex[:]]
        sum_sg = [early_sg[:, 0, :], early_sg[:, 1, :], third[:, 1, :], last_sg[:]]
        for b in range(BLOCKS):
            add_turned(sum_ex[b], ex[b], range(D))
            add_turned(sum_sg[b], sg[b], range(D))

        both = [late.tile([P, 2, P], F32, name="both%d" % b, offset=BOTH_AT + 8 * P * b, align_bytes=64) for b in range(BLOCKS)]
        runs = [range(b, b + 1) for b in range(BLOCKS)]
        back = [psum.tile([P, 1, 2, V], F32, name="back%d" % b, tag="bank%d" % (BLOCKS + b if b else 0)) for b in range(BLOCKS)]
        back_of = {b: back[b][:, 0] for b in range(BLOCKS)}

        def scale_total(b):
            nc.vector.tensor_scalar(
                both[b][:, 0], sum_ex[b], half_one[:], 2.0 * EPS * math.exp(KNEE), ALU.mult, ALU.mult
            )

        def add_total(b):
            nc.vector.tensor_tensor(both[b][:, 1], sum_sg[b], both[b][:, 0], ALU.add)
            for i in range(2):
                nc.tensor.transpose(back_of[b][:, i, :], both[b][:, i, :], ident[:])

        scale_total(0)
        for b in range(1, BLOCKS):
            scale_total(b)
            add_total(b - 1)
        add_total(last)
        out_rows = out.rearrange("(b p) v -> p b v", p=P)
        for r, run in enumerate(runs):
            logs = keep.tile([P, len(run), 2, V], F32, name="logs%d" % r)
            nc.scalar.activation(out=logs[:], in_=back[r][:], func=ACT.Ln)
            res = keep.tile([P, len(run), V], F32, name="res%d" % r)
            nc.vector.scalar_tensor_tensor(res[:], logs[:, :, 0], -math.log(EPS), logs[:, :, 1], ALU.add, ALU.subtract)
            nc.sync.dma_start(out=out_rows[:, run.start : run.stop, :], in_=res[:])
